import numpy as np
import ml_dtypes


def mxq(x, axis, fmt="e4m3"):
    dtype, down = {"e4m3": (ml_dtypes.float8_e4m3fn, 7), "e5m2": (ml_dtypes.float8_e5m2, 14)}[fmt]
    v = np.moveaxis(np.asarray(x, np.float32).astype(ml_dtypes.bfloat16).astype(np.float64), axis, -1)
    blocks = v.reshape(v.shape[:-1] + (-1, 32))
    amax = np.abs(blocks).max(-1, keepdims=True)
    byte = np.maximum(np.where(amax > 0, np.frexp(amax)[1] - 1 + 127, 0) - down, 1)
    scale = np.exp2(byte - 127.0)
    codes = (blocks / scale).astype(np.float32).astype(dtype).astype(np.float64)
    return np.moveaxis((codes * scale).reshape(v.shape), -1, axis)


WIDE = False


def mx_kscale(k):
    if not WIDE:
        return np.ones(k)
    levels = np.array([10, -10, 5, -5, 0])
    if k % 512:
        return np.exp2(np.random.permutation(np.resize(levels, k // 32))).repeat(32)
    a = np.empty((k // 512, 16))
    for p in range(k // 512):
        a[p, :8] = np.random.permutation(np.resize(levels, 8))
        for g in range(8):
            far = levels[np.abs(levels - a[p, g]) >= 10]
            a[p, g + 8] = far[np.random.randint(len(far))]
    return np.exp2(a.ravel()).repeat(32)


def f64(x):
    return np.asarray(x).astype(np.float64)


def striped(idx):
    return np.tile(idx.reshape(-1, 16).T, (8, 1)).astype(np.uint16)


def unstriped(offs):
    return offs[:16].T.reshape(-1).astype(np.int64)


E2M1 = np.array([0.0, 0.5, 1.0, 1.5, 2.0, 3.0, 4.0, 6.0, -0.0, -0.5, -1.0, -1.5, -2.0, -3.0, -4.0, -6.0])


def pack_weight(w, fmt):
    k, n = w.shape
    w = f64(np.asarray(w, np.float32).astype(ml_dtypes.bfloat16)).reshape(k // 32, 32, n)
    amax = np.abs(w).max(1)
    if fmt == "e4m3":
        byte = np.frexp(amax)[1] - 1 + 127 - 7
    else:
        mant, ex = np.frexp(amax / 6.0)
        byte = np.where(mant > 0.5, ex, ex - 1) + 127
    byte = np.clip(np.where(amax > 0, byte, 1), 1, 254)
    scaled = (w * np.exp2(127.0 - byte)[:, None, :]).reshape(k, n).astype(np.float32)
    by_word = np.ascontiguousarray(scaled.reshape(k // 512, 128, 4, n).transpose(0, 1, 3, 2))
    if fmt == "e4m3":
        words = by_word.astype(ml_dtypes.float8_e4m3fn).view(np.uint8)
    else:
        c = by_word.astype(ml_dtypes.float4_e2m1fn).view(np.uint8) & 0xF
        words = (c[..., 0::2] | (c[..., 1::2] << 4)).reshape(k // 512, 128, 2 * n)
    return np.ascontiguousarray(words), np.ascontiguousarray(byte.astype(np.uint8).reshape(k // 512, 16, n))


def unpack_weight(words, scales, fmt):
    g, _, n = scales.shape
    words = np.ascontiguousarray(words).reshape(g, 128, n, -1)
    if fmt == "e4m3":
        vals = words.view(ml_dtypes.float8_e4m3fn).astype(np.float64)
    else:
        nib = np.empty((g, 128, n, 4), np.uint8)
        nib[..., 0::2] = words & 0xF
        nib[..., 1::2] = words >> 4
        vals = E2M1[nib]
    vals = vals * np.repeat(np.exp2(scales.astype(np.float64) - 127.0), 8, axis=1)[..., None]
    return vals.transpose(0, 1, 3, 2).reshape(g * 512, n)


def gelu(v):
    return 0.5 * v * (1.0 + np.tanh(np.sqrt(2.0 / np.pi) * (v + 0.044715 * v**3)))


def striped8(idx):
    return np.concatenate([v.reshape(-1, 16).T for v in idx]).astype(np.uint16)


def unstriped8(offs):
    return np.stack([offs[16 * g:16 * g + 16].T.reshape(-1) for g in range(8)]).astype(np.int64)


def heads(h, wgt, idx8):
    r = np.arange(h.shape[0])
    return wgt[r // 4 % 128] * h[r[:, None], idx8[r % 512 // 64]]


def bf(x):
    return np.asarray(x, np.float32).astype(ml_dtypes.bfloat16)


def planes(Y):
    n, m = Y.shape
    b = f64(bf(Y)).reshape(n // 32, 32, m)
    amax = np.abs(b).max(1)
    byte = np.clip(np.where(amax > 0, np.frexp(amax)[1] - 1 + 127 - 7, 1), 1, 254)
    codes = (b * np.exp2(127.0 - byte)[:, None, :]).reshape(n, m).astype(np.float32).astype(ml_dtypes.float8_e4m3fn).view(np.uint8)
    words = codes.reshape(n // 512, 128, 4, m).transpose(0, 1, 3, 2)
    return np.ascontiguousarray(words), np.ascontiguousarray(byte.astype(np.uint8).reshape(n // 512, 16, m))


T, S, P, K, F, H, N = 2048, 1024, 512, 512, 512, 1024, 512

def setup_inputs():
    n = np.random.standard_normal
    s, q, u = mx_kscale(K)[:, None], mx_kscale(F)[:, None], mx_kscale(H)[:, None]
    tab_words, tab_scales = pack_weight(n((K, T)) * s, "e4m3")
    wc_words, wc_scales = pack_weight(0.6 * n((K, H)) / np.sqrt(K) / s, "e2m1")
    ug_words, ug_scales = pack_weight(0.9 * n((H, H)) / np.sqrt(H) / u, "e4m3")
    return {
        "tab_words": tab_words, "tab_scales": tab_scales,
        "offs": striped(np.random.permutation(T)[:S]),
        "offs2": striped8(np.stack([np.random.permutation(S)[:P] for _ in range(8)])),
        "wgt": np.repeat(np.random.uniform(0.5, 2.0, (8, P)), 16, axis=0).astype(np.float32),
        "wc_words": wc_words, "wc_scales": wc_scales,
        "ug_words": ug_words, "ug_scales": ug_scales,
        "us": (0.6 * n((H, H)) / np.sqrt(H) / u).astype(np.float32),
        "wp": (0.9 * n((F, H)) / np.sqrt(F) / q).astype(np.float32),
        "wo": (n((H, N)) / np.sqrt(H) / u * np.exp(0.8 * n(N))).astype(np.float32),
        "st": (n((H, P)) * u).astype(np.float32),
        "pros": (n((F, P)) * q).astype(np.float32),
        "gain": (np.random.uniform(0.5, 1.5, H) * u[:, 0]).astype(np.float32),
    }

def reference(tab_words, tab_scales, offs, offs2, wgt, wc_words, wc_scales, ug_words, ug_scales, us, wp, wo, st, pros, gain):
    v = unpack_weight(tab_words, tab_scales, "e4m3")[:, unstriped(offs)]
    h = unpack_weight(wc_words, wc_scales, "e2m1").T @ v
    x = heads(h, f64(wgt), unstriped8(offs2))
    stq = mxq(f64(st), 0, "e4m3")
    cand = np.tanh(x + (mxq(f64(us), 0, "e4m3").T @ stq))
    zg = (unpack_weight(ug_words, ug_scales, "e4m3").T @ stq
               + mxq(f64(wp), 0, "e4m3").T @ mxq(f64(pros), 0, "e4m3"))
    keep = 1.0 / (1.0 + np.exp(-zg))
    new = keep * f64(st) + f64(gain)[:, None] * cand
    y = mxq(f64(wo), 0, "e4m3").T @ mxq(new, 0, "e4m3")
    words, scales = planes(y)
    return y, words, scales

@@ -1,0 +1,242 @@
+from contextlib import ExitStack
+
+import concourse.mybir as mybir
+
+T, S, M, K, H, N = 2048, 1024, 512, 512, 1024, 512
+FLOPS = 2 * (K * H * S + 2 * H * H * M + K * H * M + H * N * M)
+
+F32 = mybir.dt.float32
+BF16 = mybir.dt.bfloat16
+I32 = mybir.dt.int32
+U32 = mybir.dt.uint32
+U16 = mybir.dt.uint16
+U8 = mybir.dt.uint8
+FP8X4 = mybir.dt.float8_e4m3fn_x4
+FP4X4 = mybir.dt.float4_e2m1fn_x4
+ACT = mybir.ActivationFunctionType
+MULT = mybir.AluOpType.mult
+ADD = mybir.AluOpType.add
+
+P = 128
+W = 512
+HALF = 256
+LOADS = ["st00", "st10", "ug", "pr00", "wp00", "wp01", "us00", "us01", "us10", "us11", "wo00", "wo10"]
+PREP = ["st0", "st1", "ug", "pr", "wp", "us0", "us1", "z0", "z1", "c0", "A0", "c1", "A1", "wo"]
+U_ORDER = (0, 1)
+PIECES = {"st0": ["st00"], "st1": ["st10"], "pr": ["pr00"], "wp": ["wp00", "wp01"], "us0": ["us00", "us01"], "us1": ["us10", "us11"], "wo": ["wo00", "wo10"]}
+ON_VECTOR = ["st00", "us10", "us11"]
+NEW_WEAVE = ["scalar", "scalar", "scalar", "vector"]
+HBUFS = 7
+RAWBUFS = 7
+STAGE = {"scalar": 4, "vector": 2}
+BANKS = {"h": 4, "u": 2, "z": 2}
+
+
+def tile_list_voice_state_step_kernel(
+    tc, tab_words, tab_scales, offs, offs2, wgt, wc_words, wc_scales, ug_words, ug_scales,
+    us, wp, wo, st, pros, gain, out_0, out_1, out_2,
+):
+    nc = tc.nc
+    with ExitStack() as ctx:
+        held = ctx.enter_context(tc.tile_pool(name="held", bufs=1))
+        ring = ctx.enter_context(tc.tile_pool(name="ring", bufs=1))
+        psum = ctx.enter_context(tc.psum_pool(name="psum", bufs=1))
+
+        def raw_tile(shape, dtype, name):
+            return ring.tile(shape, dtype, name=name, tag="raw", bufs=RAWBUFS, align_bytes=64)
+
+        def keep_tile(shape, dtype, name):
+            return held.tile(shape, dtype, name=name, align_bytes=64)
+
+        def bank(name, tag):
+            return psum.tile([P, W], F32, name=name, tag="bank", bufs=8)
+
+        tab_sc = keep_tile([P, T], U8, "tab_sc")
+        wc_sc = keep_tile([P, H], U8, "wc_sc")
+        ug_sc = keep_tile([P, H], U8, "ug_sc")
+        nc.gpsimd.memset(wc_sc[:].bitcast(I32), 0)
+        nc.gpsimd.memset(ug_sc[:].bitcast(I32), 0)
+        warm = keep_tile([P, 8], F32, "warm")
+        nc.gpsimd.memset(warm[:, 0:1], 0.0)
+        nc.scalar.activation(out=warm[:, 4:5], in_=warm[:, 0:1], func=ACT.Sigmoid)
+
+        list1 = held.tile([P, S // 16], U16, name="list1")
+        list2 = held.tile([P, M // 16], U16, name="list2")
+        nc.sync.dma_start(list1[:], offs)
+        wc_raw = keep_tile([P, 2 * H], U8, "wc_raw")
+        nc.sync.dma_start(out=wc_raw[:].bitcast(I32), in_=wc_words[0].bitcast(I32))
+        for q in range(4):
+            nc.sync.dma_start(out=tab_sc[32 * q : 32 * q + 32, :].bitcast(I32), in_=tab_scales[0, 4 * q : 4 * q + 4, :].bitcast(I32).partition_broadcast(8))
+        tab_raw = raw_tile([P, T], I32, "tab_raw")
+        nc.sync.dma_start(out=tab_raw[:], in_=tab_words[0].rearrange("p t i -> p (t i)").bitcast(I32))
+        for q in range(4):
+            nc.sync.dma_start(out=wc_sc[32 * q : 32 * q + 4, :].bitcast(I32), in_=wc_scales[0, 4 * q : 4 * q + 4, :].bitcast(I32))
+
+        def load_rows(tile, src, a, b):
+            nc.sync.dma_start(out=tile[:], in_=src[W * a : W * (a + 1), W * b : W * (b + 1)].rearrange("(p j) c -> p j c", j=4))
+            return tile
+
+        nc.sync.dma_start(list2[:], offs2)
+        wgt_sb = keep_tile([P, M], F32, "wgt_sb")
+        nc.sync.dma_start(out=wgt_sb[:], in_=wgt)
+        raw = {}
+        gain_sb = keep_tile([P, 2, 4], F32, "gain_sb")
+        sources = {"st": st, "us": us, "wp": wp, "wo": wo, "pr": pros}
+        for name in LOADS:
+            if name == "ug":
+                for q in range(4):
+                    nc.sync.dma_start(out=ug_sc[32 * q : 32 * q + 8, :].bitcast(I32), in_=ug_scales[:, 4 * q : 4 * q + 4, :].bitcast(I32))
+                nc.sync.dma_start(out=gain_sb[:], in_=gain.rearrange("(b p t) -> p b t", b=2, t=4))
+                ug_raw = raw_tile([P, 2 * H], I32, "ug_raw")
+                nc.sync.dma_start(out=ug_raw[:].rearrange("p (a c) -> p a c", a=2), in_=ug_words.rearrange("a p c i -> p a (c i)").bitcast(I32))
+            else:
+                make = keep_tile if name[:2] == "st" else raw_tile
+                raw[name] = load_rows(make([P, 4, W], F32, name), sources[name[:2]], int(name[2]), int(name[3]))
+        st_raw = [raw["st00"], raw["st10"]]
+
+        def copy_on(engine, out, in_):
+            if engine == "vector":
+                nc.vector.tensor_copy(out=out, in_=in_)
+            else:
+                nc.scalar.copy(out=out, in_=in_)
+
+        def stage_tile(engine, width, name):
+            return ring.tile([P, width], BF16, name=name, tag="stage_" + engine, bufs=STAGE[engine], align_bytes=64)
+
+        def weave(engine, out, planes):
+            copy_on(engine, out.rearrange("p (c i j) -> p c j i", i=4, j=4), planes.rearrange("p j (c i) -> p c j i", i=4))
+
+        def deal(engine, out, planes):
+            copy_on(engine, out.rearrange("p (t m j) -> p m j t", t=4, j=4), planes.rearrange("p j (m t) -> p m j t", t=4))
+
+        def quantise(rounded, name):
+            width = rounded[:].shape[1] // 4
+            codes = keep_tile([P, width], U32, name + "_codes")
+            scales = keep_tile([P, width], U8, name + "_scales")
+            nc.vector.quantize_mx(out=codes[:].bitcast(FP8X4), scales=scales[:], in_=rounded[:])
+            return codes, scales
+
+        def prepare(layout, names, name):
+            rounded = stage_tile("scalar" if len(names) == 2 else "vector", 4 * W * len(names), name + "_bf")
+            for i, piece in enumerate(names):
+                layout("vector" if piece in ON_VECTOR else "scalar", rounded[:, 4 * W * i : 4 * W * (i + 1)], raw[piece][:])
+            return quantise(rounded, name)
+
+        wc_codes, wc_scd, v_words, v_sc = [], [], [], []
+        for s in range(2):
+            codes = keep_tile([P, 2 * W], U8, f"wc_codes{s}")
+            nc.vector.tensor_copy(
+                out=codes[:].rearrange("p (t m e) -> p t m e", t=4, e=2),
+                in_=wc_raw[:, 2 * W * s : 2 * W * (s + 1)].rearrange("p (m t e) -> p t m e", t=4, e=2),
+            )
+            wc_codes.append(codes)
+            scales = keep_tile([P, W], U8, f"wc_scd{s}")
+            nc.vector.tensor_copy(
+                out=scales[:].rearrange("p (t m) -> p t m", t=4),
+                in_=wc_sc[:, W * s : W * (s + 1)].rearrange("p (m t) -> p t m", t=4),
+            )
+            wc_scd.append(scales)
+            picked = keep_tile([P, W], U32, f"v_words{s}")
+            nc.vector.tensor_copy(out=picked[:], in_=tab_raw[:].bitcast(U32).indirect(list1[:, 32 * s : 32 * (s + 1)]))
+            v_words.append(picked)
+            picked = keep_tile([P, W], U8, f"v_sc{s}")
+            nc.vector.tensor_copy(out=picked[:], in_=tab_sc[:].indirect(list1[:, 32 * s : 32 * (s + 1)]))
+            v_sc.append(picked)
+
+        x = [keep_tile([P, 4, M], F32, f"x{b}") for b in range(2)]
+        for b in range(2):
+            h = [ring.tile([P, S], F32, name=f"h{b}{t}", tag="h", bufs=HBUFS, align_bytes=64) for t in range(4)]
+            for s in range(2):
+                for t in range(4):
+                    acc = bank(f"hacc{b}{t}{s}", "h")
+                    nc.tensor.matmul_mx(
+                        out=acc[:],
+                        lhsT=wc_codes[b][:, 2 * P * t : 2 * P * (t + 1)].bitcast(FP4X4), lhsT_scale=wc_scd[b][:, P * t : P * (t + 1)],
+                        rhs=v_words[s][:].bitcast(FP8X4), rhs_scale=v_sc[s][:],
+                        start=True, stop=True,
+                    )
+                    nc.scalar.copy(out=h[t][:, W * s : W * (s + 1)], in_=acc[:])
+            for t in range(4):
+                nc.vector.tensor_tensor(out=x[b][:, t, :], in0=h[t][:].indirect(list2[:]), in1=wgt_sb[:], op=MULT)
+
+        def product(acc, lhs, lhs_cols, rhs, rhs_cols, start, stop, lhs_scale=None):
+            nc.tensor.matmul_mx(
+                out=acc, lhsT=lhs[0][:, lhs_cols].bitcast(FP8X4), lhsT_scale=lhs[1][:, lhs_cols] if lhs_scale is None else lhs_scale,
+                rhs=rhs[0][:, rhs_cols].bitcast(FP8X4), rhs_scale=rhs[1][:, rhs_cols], start=start, stop=stop,
+            )
+
+        ug_codes = keep_tile([P, 2 * H], I32, "ug_codes")
+        ug_scd = keep_tile([P, H], U8, "ug_scd")
+        made = {}
+        keep = {}
+        whole = slice(0, W)
+        for name in PREP:
+            if name == "ug":
+                nc.vector.tensor_copy(
+                    out=ug_codes[:].rearrange("p (g t m) -> p g m t", g=4, t=4),
+                    in_=ug_raw[:].rearrange("p (g m t) -> p g m t", g=4, t=4),
+                )
+                nc.vector.tensor_copy(
+                    out=ug_scd[:].rearrange("p (b t m) -> p b t m", b=2, t=4),
+                    in_=ug_sc[:].rearrange("p (b m t) -> p b t m", b=2, t=4),
+                )
+            elif name[0] == "z":
+                b = int(name[1])
+                for t in range(4):
+                    cols = slice(W * b + P * t, W * b + P * (t + 1))
+                    acc = bank(f"z{b}{t}", "z")
+                    product(acc[:], made["wp"], cols, made["pr"], whole, True, False)
+                    for a in range(2):
+                        product(acc[:], (ug_codes, None), slice(H * a + cols.start, H * a + cols.stop), made[f"st{a}"], whole, False, a == 1, ug_scd[4 * a :, cols])
+                    kept = keep_tile([P, M], F32, f"keep{b}{t}")
+                    nc.scalar.activation(out=kept[:], in_=acc[:], func=ACT.Sigmoid)
+                    keep[b, t] = kept
+            elif name[0] == "c":
+                b = int(name[1])
+                for t in range(4):
+                    cols = slice(W * b + P * t, W * b + P * (t + 1))
+                    acc = bank(f"u{b}{t}", "u")
+                    for a in U_ORDER:
+                        product(acc[:], made[f"us{a}"], cols, made[f"st{a}"], whole, a == U_ORDER[0], a == U_ORDER[1])
+                    nc.vector.tensor_tensor(out=x[b][:, t, :], in0=acc[:], in1=x[b][:, t, :], op=ADD)
+                    nc.scalar.activation(out=x[b][:, t, :], in_=x[b][:, t, :], func=ACT.Tanh)
+            elif name[0] == "A":
+                b = int(name[1])
+                for t in range(4):
+                    nc.vector.tensor_tensor(out=keep[b, t][:], in0=keep[b, t][:], in1=st_raw[b][:, t, :], op=MULT)
+            else:
+                made[name] = prepare(weave if name[:2] in ("st", "pr") else deal, PIECES[name], name)
+        wo_q = made["wo"]
+
+        y_scales = keep_tile([P, M], U8, "y_scales")
+        y_rows = out_0.rearrange("(p t) m -> p t m", t=4)
+        y_words = out_1[0].rearrange("p m t -> p (m t)").bitcast(I32)
+        for s in range(2):
+            cols = slice(HALF * s, HALF * (s + 1))
+            new_q = []
+            for b in range(2):
+                planes = ring.tile([P, 4, HALF], BF16, name=f"new{b}{s}", tag="h", bufs=HBUFS, align_bytes=64)
+                for t in range(4):
+                    nc.vector.scalar_tensor_tensor(
+                        out=planes[:, t, :], in0=x[b][:, t, cols], scalar=gain_sb[:, b, t : t + 1],
+                        in1=keep[b, t][:, cols], op0=MULT, op1=ADD,
+                    )
+                rounded = stage_tile("scalar", 4 * HALF, f"new_bf{b}{s}")
+                weave(NEW_WEAVE[2 * s + b], rounded[:], planes[:])
+                new_q.append(quantise(rounded, f"newq{b}{s}"))
+            y = ring.tile([P, 4, HALF], F32, name=f"y{s}", tag="h", bufs=HBUFS, align_bytes=64)
+            for u in range(2):
+                acc = bank(f"y{s}{u}", "h")
+                for e in range(2):
+                    t = 2 * u + e
+                    for b in range(2):
+                        product(acc[:, HALF * e : HALF * (e + 1)], wo_q, slice(W * b + P * t, W * b + P * (t + 1)), new_q[b], slice(0, HALF), b == 0, b == 1)
+                nc.scalar.copy(out=y[:, 2 * u : 2 * u + 2, :].rearrange("p e m -> p (e m)"), in_=acc[:])
+            nc.sync.dma_start(out=y_rows[:, :, cols], in_=y[:])
+            rounded = stage_tile("vector", 4 * HALF, f"y_bf{s}")
+            weave("vector", rounded[:], y[:])
+            y_codes = keep_tile([P, HALF], I32, f"y_codes{s}")
+            nc.vector.quantize_mx(out=y_codes[:].bitcast(FP8X4), scales=y_scales[:, cols], in_=rounded[:])
+            nc.sync.dma_start(out=y_words[:, cols], in_=y_codes[:])
+        for q in range(4):
+            nc.sync.dma_start(out=out_2[0, 4 * q : 4 * q + 4, :].bitcast(I32), in_=y_scales[32 * q : 32 * q + 4, :].bitcast(I32))

@@ -1,6 +1,7 @@
 from contextlib import ExitStack
 
 import concourse.mybir as mybir
+from concourse.masks import make_identity
 
 T, S, M, K, H, N = 2048, 1024, 512, 512, 1024, 512
 FLOPS = 2 * (K * H * S + 2 * H * H * M + K * H * M + H * N * M)
@@ -20,15 +21,16 @@ ADD = mybir.AluOpType.add
 P = 128
 W = 512
 HALF = 256
-LOADS = ["st00", "st10", "ug", "pr00", "wp00", "wp01", "us00", "us01", "us10", "us11", "wo00", "wo10"]
-PREP = ["st0", "st1", "ug", "pr", "wp", "us0", "us1", "z0", "z1", "c0", "A0", "c1", "A1", "wo"]
-U_ORDER = (0, 1)
-PIECES = {"st0": ["st00"], "st1": ["st10"], "pr": ["pr00"], "wp": ["wp00", "wp01"], "us0": ["us00", "us01"], "us1": ["us10", "us11"], "wo": ["wo00", "wo10"]}
-ON_VECTOR = ["st00", "us10", "us11"]
-NEW_WEAVE = ["scalar", "scalar", "scalar", "vector"]
+LOADS = ["st00", "wgt", "st10", "ug", "wp00", "wp01", "us00", "us10", "us01", "us11", "wo00", "wo10"]
+PREP = ["pr00", "h0", "st00", "st10", "wp00", "h1", "z0", "wp01", "us00", "us10", "z1", "A0", "us01", "us11", "wo00", "c0", "A1", "wo10", "c1", "n00", "n10", "n01", "y0", "n11", "y1"]
+U_ORDER = (1, 0)
+ON_VECTOR = ["st00", "wp01", "us01", "n11", "e11", "e13", "y1", "y0"]
+CHUNKS = [(0, 256), (256, 512)]
+Y_PER_BANK = [1, 1]
+TURNED = 4
 HBUFS = 7
-RAWBUFS = 7
-STAGE = {"scalar": 4, "vector": 2}
+RAWBUFS = 6
+STAGE = 8
 BANKS = {"h": 4, "u": 2, "z": 2}
 
 
@@ -54,11 +56,13 @@ def tile_list_voice_state_step_kernel(
         tab_sc = keep_tile([P, T], U8, "tab_sc")
         wc_sc = keep_tile([P, H], U8, "wc_sc")
         ug_sc = keep_tile([P, H], U8, "ug_sc")
-        nc.gpsimd.memset(wc_sc[:].bitcast(I32), 0)
         nc.gpsimd.memset(ug_sc[:].bitcast(I32), 0)
         warm = keep_tile([P, 8], F32, "warm")
         nc.gpsimd.memset(warm[:, 0:1], 0.0)
         nc.scalar.activation(out=warm[:, 4:5], in_=warm[:, 0:1], func=ACT.Sigmoid)
+
+        ident = keep_tile([P, P], F32, "ident")
+        make_identity(nc, ident[:])
 
         list1 = held.tile([P, S // 16], U16, name="list1")
         list2 = held.tile([P, M // 16], U16, name="list2")
@@ -67,27 +71,32 @@ def tile_list_voice_state_step_kernel(
         nc.sync.dma_start(out=wc_raw[:].bitcast(I32), in_=wc_words[0].bitcast(I32))
         for q in range(4):
             nc.sync.dma_start(out=tab_sc[32 * q : 32 * q + 32, :].bitcast(I32), in_=tab_scales[0, 4 * q : 4 * q + 4, :].bitcast(I32).partition_broadcast(8))
+        pros_rows = pros.rearrange("(p j) c -> p j c", j=4)
+        pros_raw = [keep_tile([P, 4, HALF], F32, f"pros{s}") for s in range(2)]
+        nc.sync.dma_start(out=pros_raw[0][:], in_=pros_rows[:, :, 0:HALF])
         tab_raw = raw_tile([P, T], I32, "tab_raw")
         nc.sync.dma_start(out=tab_raw[:], in_=tab_words[0].rearrange("p t i -> p (t i)").bitcast(I32))
         for q in range(4):
-            nc.sync.dma_start(out=wc_sc[32 * q : 32 * q + 4, :].bitcast(I32), in_=wc_scales[0, 4 * q : 4 * q + 4, :].bitcast(I32))
+            nc.sync.dma_start(out=wc_sc[32 * q : 32 * q + 32, :].bitcast(I32), in_=wc_scales[0, 4 * q : 4 * q + 4, :].bitcast(I32).partition_broadcast(8))
 
         def load_rows(tile, src, a, b):
             nc.sync.dma_start(out=tile[:], in_=src[W * a : W * (a + 1), W * b : W * (b + 1)].rearrange("(p j) c -> p j c", j=4))
             return tile
 
-        nc.sync.dma_start(list2[:], offs2)
+        nc.sync.dma_start(out=pros_raw[1][:], in_=pros_rows[:, :, HALF:M])
         wgt_sb = keep_tile([P, M], F32, "wgt_sb")
-        nc.sync.dma_start(out=wgt_sb[:], in_=wgt)
         raw = {}
         gain_sb = keep_tile([P, 2, 4], F32, "gain_sb")
         sources = {"st": st, "us": us, "wp": wp, "wo": wo, "pr": pros}
         for name in LOADS:
-            if name == "ug":
+            if name == "wgt":
+                nc.sync.dma_start(list2[:], offs2)
+                nc.sync.dma_start(out=wgt_sb[:], in_=wgt)
+            elif name == "ug":
                 for q in range(4):
                     nc.sync.dma_start(out=ug_sc[32 * q : 32 * q + 8, :].bitcast(I32), in_=ug_scales[:, 4 * q : 4 * q + 4, :].bitcast(I32))
                 nc.sync.dma_start(out=gain_sb[:], in_=gain.rearrange("(b p t) -> p b t", b=2, t=4))
-                ug_raw = raw_tile([P, 2 * H], I32, "ug_raw")
+                ug_raw = keep_tile([P, 2 * H], I32, "ug_raw")
                 nc.sync.dma_start(out=ug_raw[:].rearrange("p (a c) -> p a c", a=2), in_=ug_words.rearrange("a p c i -> p a (c i)").bitcast(I32))
             else:
                 make = keep_tile if name[:2] == "st" else raw_tile
@@ -101,7 +110,7 @@ def tile_list_voice_state_step_kernel(
                 nc.scalar.copy(out=out, in_=in_)
 
         def stage_tile(engine, width, name):
-            return ring.tile([P, width], BF16, name=name, tag="stage_" + engine, bufs=STAGE[engine], align_bytes=64)
+            return ring.tile([P, width], BF16, name=name, tag="stage", bufs=STAGE, align_bytes=64)
 
         def weave(engine, out, planes):
             copy_on(engine, out.rearrange("p (c i j) -> p c j i", i=4, j=4), planes.rearrange("p j (c i) -> p c j i", i=4))
@@ -144,7 +153,7 @@ def tile_list_voice_state_step_kernel(
             v_sc.append(picked)
 
         x = [keep_tile([P, 4, M], F32, f"x{b}") for b in range(2)]
-        for b in range(2):
+        def traits(b):
             h = [ring.tile([P, S], F32, name=f"h{b}{t}", tag="h", bufs=HBUFS, align_bytes=64) for t in range(4)]
             for s in range(2):
                 for t in range(4):
@@ -165,78 +174,92 @@ def tile_list_voice_state_step_kernel(
                 rhs=rhs[0][:, rhs_cols].bitcast(FP8X4), rhs_scale=rhs[1][:, rhs_cols], start=start, stop=stop,
             )
 
-        ug_codes = keep_tile([P, 2 * H], I32, "ug_codes")
-        ug_scd = keep_tile([P, H], U8, "ug_scd")
+        y_scales = keep_tile([P, M], U8, "y_scales")
+        y_rows = out_0.rearrange("(p t) m -> p t m", t=4)
+        y_words = out_1[0].rearrange("p m t -> p (m t)").bitcast(I32)
+        new_q = {}
+
+        def blend(b, s):
+            cols = slice(*CHUNKS[s])
+            wide = cols.stop - cols.start
+            planes = ring.tile([P, 4, wide], BF16, name=f"new{b}{s}", tag="h", bufs=HBUFS, align_bytes=64)
+            for t in range(4):
+                nc.vector.scalar_tensor_tensor(
+                    out=planes[:, t, :], in0=x[b][:, t, cols], scalar=gain_sb[:, b, t : t + 1],
+                    in1=keep[b, t][:, cols], op0=MULT, op1=ADD,
+                )
+            rounded = stage_tile("scalar", 4 * wide, f"new_bf{b}{s}")
+            weave("vector" if f"n{b}{s}" in ON_VECTOR else "scalar", rounded[:], planes[:])
+            new_q[b, s] = quantise(rounded, f"newq{b}{s}")
+
+        def finish(s):
+            cols = slice(*CHUNKS[s])
+            wide = cols.stop - cols.start
+            y = ring.tile([P, 4, wide], F32, name=f"y{s}", tag="h", bufs=HBUFS, align_bytes=64)
+            per = Y_PER_BANK[s]
+            for u in range(4 // per):
+                acc = bank(f"y{s}{u}", "h")
+                for e in range(per):
+                    t = per * u + e
+                    for b in range(2):
+                        product(acc[:, wide * e : wide * (e + 1)], made[f"wo{b}0"], slice(P * t, P * (t + 1)), new_q[b, s], slice(0, wide), b == 0, b == 1)
+                copy_on("vector" if f"e{s}{u}" in ON_VECTOR else "scalar", y[:, per * u : per * (u + 1), :].rearrange("p e m -> p (e m)"), acc[:, 0 : wide * per])
+            nc.sync.dma_start(out=y_rows[:, :, cols], in_=y[:])
+            rounded = stage_tile("vector", 4 * wide, f"y_bf{s}")
+            weave("vector" if f"y{s}" in ON_VECTOR else "scalar", rounded[:], y[:])
+            y_codes = keep_tile([P, wide], I32, f"y_codes{s}")
+            nc.vector.quantize_mx(out=y_codes[:].bitcast(FP8X4), scales=y_scales[:, cols], in_=rounded[:])
+            nc.sync.dma_start(out=y_words[:, cols], in_=y_codes[:])
+
         made = {}
         keep = {}
+        turned = {}
         whole = slice(0, W)
         for name in PREP:
-            if name == "ug":
-                nc.vector.tensor_copy(
-                    out=ug_codes[:].rearrange("p (g t m) -> p g m t", g=4, t=4),
-                    in_=ug_raw[:].rearrange("p (g m t) -> p g m t", g=4, t=4),
-                )
-                nc.vector.tensor_copy(
-                    out=ug_scd[:].rearrange("p (b t m) -> p b t m", b=2, t=4),
-                    in_=ug_sc[:].rearrange("p (b m t) -> p b t m", b=2, t=4),
-                )
+            if name == "pr00":
+                rounded = stage_tile("scalar", 4 * W, "pros_bf")
+                for s in range(2):
+                    weave("scalar", rounded[:, 4 * HALF * s : 4 * HALF * (s + 1)], pros_raw[s][:])
+                made[name] = quantise(rounded, name)
+            elif name[0] == "h":
+                traits(int(name[1]))
+            elif name[0] == "n":
+                blend(int(name[1]), int(name[2]))
+            elif name[0] == "y":
+                finish(int(name[1]))
             elif name[0] == "z":
                 b = int(name[1])
-                for t in range(4):
-                    cols = slice(W * b + P * t, W * b + P * (t + 1))
-                    acc = bank(f"z{b}{t}", "z")
-                    product(acc[:], made["wp"], cols, made["pr"], whole, True, False)
+                for g in range(4):
+                    cols = slice(P * g, P * (g + 1))
+                    acc = bank(f"z{b}{g}", "z")
+                    product(acc[:], made["pr00"], cols, made[f"wp0{b}"], whole, True, False)
                     for a in range(2):
-                        product(acc[:], (ug_codes, None), slice(H * a + cols.start, H * a + cols.stop), made[f"st{a}"], whole, False, a == 1, ug_scd[4 * a :, cols])
-                    kept = keep_tile([P, M], F32, f"keep{b}{t}")
-                    nc.scalar.activation(out=kept[:], in_=acc[:], func=ACT.Sigmoid)
-                    keep[b, t] = kept
+                        nc.tensor.matmul_mx(
+                            out=acc[:], lhsT=made[f"st{a}0"][0][:, cols].bitcast(FP8X4), lhsT_scale=made[f"st{a}0"][1][:, cols],
+                            rhs=ug_raw[:, H * a + W * b : H * a + W * (b + 1)].bitcast(FP8X4), rhs_scale=ug_sc[4 * a :, W * b : W * (b + 1)],
+                            start=False, stop=(a == 1),
+                        )
+                    turned[b, g] = ring.tile([P, 4, P], F32, name=f"turned{b}{g}", tag="turned", bufs=TURNED, align_bytes=64)
+                    nc.scalar.activation(out=turned[b, g][:], in_=acc[:].rearrange("m (p t) -> m t p", t=4), func=ACT.Sigmoid)
             elif name[0] == "c":
                 b = int(name[1])
                 for t in range(4):
                     cols = slice(W * b + P * t, W * b + P * (t + 1))
                     acc = bank(f"u{b}{t}", "u")
                     for a in U_ORDER:
-                        product(acc[:], made[f"us{a}"], cols, made[f"st{a}"], whole, a == U_ORDER[0], a == U_ORDER[1])
+                        product(acc[:], made[f"us{a}{b}"], slice(P * t, P * (t + 1)), made[f"st{a}0"], whole, a == U_ORDER[0], a == U_ORDER[1])
                     nc.vector.tensor_tensor(out=x[b][:, t, :], in0=acc[:], in1=x[b][:, t, :], op=ADD)
                     nc.scalar.activation(out=x[b][:, t, :], in_=x[b][:, t, :], func=ACT.Tanh)
             elif name[0] == "A":
                 b = int(name[1])
                 for t in range(4):
-                    nc.vector.tensor_tensor(out=keep[b, t][:], in0=keep[b, t][:], in1=st_raw[b][:, t, :], op=MULT)
+                    acc = bank(f"k{b}{t}", "z")
+                    for g in range(4):
+                        nc.tensor.transpose(acc[:, P * g : P * (g + 1)], turned[b, g][:, t, :], ident[:])
+                    keep[b, t] = keep_tile([P, M], F32, f"keep{b}{t}")
+                    nc.vector.tensor_tensor(out=keep[b, t][:], in0=acc[:], in1=st_raw[b][:, t, :], op=MULT)
             else:
-                made[name] = prepare(weave if name[:2] in ("st", "pr") else deal, PIECES[name], name)
-        wo_q = made["wo"]
+                made[name] = prepare(weave if name[:2] in ("st", "pr", "wp") else deal, [name], name)
 
-        y_scales = keep_tile([P, M], U8, "y_scales")
-        y_rows = out_0.rearrange("(p t) m -> p t m", t=4)
-        y_words = out_1[0].rearrange("p m t -> p (m t)").bitcast(I32)
-        for s in range(2):
-            cols = slice(HALF * s, HALF * (s + 1))
-            new_q = []
-            for b in range(2):
-                planes = ring.tile([P, 4, HALF], BF16, name=f"new{b}{s}", tag="h", bufs=HBUFS, align_bytes=64)
-                for t in range(4):
-                    nc.vector.scalar_tensor_tensor(
-                        out=planes[:, t, :], in0=x[b][:, t, cols], scalar=gain_sb[:, b, t : t + 1],
-                        in1=keep[b, t][:, cols], op0=MULT, op1=ADD,
-                    )
-                rounded = stage_tile("scalar", 4 * HALF, f"new_bf{b}{s}")
-                weave(NEW_WEAVE[2 * s + b], rounded[:], planes[:])
-                new_q.append(quantise(rounded, f"newq{b}{s}"))
-            y = ring.tile([P, 4, HALF], F32, name=f"y{s}", tag="h", bufs=HBUFS, align_bytes=64)
-            for u in range(2):
-                acc = bank(f"y{s}{u}", "h")
-                for e in range(2):
-                    t = 2 * u + e
-                    for b in range(2):
-                        product(acc[:, HALF * e : HALF * (e + 1)], wo_q, slice(W * b + P * t, W * b + P * (t + 1)), new_q[b], slice(0, HALF), b == 0, b == 1)
-                nc.scalar.copy(out=y[:, 2 * u : 2 * u + 2, :].rearrange("p e m -> p (e m)"), in_=acc[:])
-            nc.sync.dma_start(out=y_rows[:, :, cols], in_=y[:])
-            rounded = stage_tile("vector", 4 * HALF, f"y_bf{s}")
-            weave("vector", rounded[:], y[:])
-            y_codes = keep_tile([P, HALF], I32, f"y_codes{s}")
-            nc.vector.quantize_mx(out=y_codes[:].bitcast(FP8X4), scales=y_scales[:, cols], in_=rounded[:])
-            nc.sync.dma_start(out=y_words[:, cols], in_=y_codes[:])
         for q in range(4):
-            nc.sync.dma_start(out=out_2[0, 4 * q : 4 * q + 4, :].bitcast(I32), in_=y_scales[32 * q : 32 * q + 4, :].bitcast(I32))
+            nc.scalar.dma_start(out=out_2[0, 4 * q : 4 * q + 4, :].bitcast(I32), in_=y_scales[32 * q : 32 * q + 4, :].bitcast(I32))

@@ -21,17 +21,18 @@ ADD = mybir.AluOpType.add
 P = 128
 W = 512
 HALF = 256
-LOADS = ["st00", "wgt", "st10", "ug", "wp00", "wp01", "us00", "us10", "us01", "us11", "wo00", "wo10"]
-PREP = ["pr00", "h0", "st00", "st10", "wp00", "h1", "z0", "wp01", "us00", "us10", "z1", "A0", "us01", "us11", "wo00", "c0", "A1", "wo10", "c1", "n00", "n10", "n01", "y0", "n11", "y1"]
-U_ORDER = (1, 0)
-ON_VECTOR = ["st00", "wp01", "us01", "n11", "e11", "e13", "y1", "y0"]
-CHUNKS = [(0, 256), (256, 512)]
-Y_PER_BANK = [1, 1]
-TURNED = 4
+HEAD = ["offs", "wc", "tsc", "offs2", "tab", "st00", "wcs", "st10", "wgt"]
+LOADS = ["pr00", "wp00", "ug", "ugs", "wp01", "us00", "us10", "us01", "us11", "gain", "wo00", "wo10"]
+PREP = ["st", "h0", "pr00", "wp00", "h1", "wp01", "us00", "z0", "us10", "us01", "z1", "A0", "us11", "c0", "wo00", "A1", "wo10", "c1", "n00", "n10", "n01", "y0", "n11", "y1"]
+ON_VECTOR = ["st10", "wp00", "us10", "us11", "n11", "e11", "e13", "y1", "y0"]
+QUEUE = {}
+U_ORDER = (0, 1)
+Z_LAST = 1
+RAWBUFS = 7
+STAGE = 6
 HBUFS = 7
-RAWBUFS = 6
-STAGE = 8
-BANKS = {"h": 4, "u": 2, "z": 2}
+TURNED = 4
+Y_PER_BANK = [1, 1]
 
 
 def tile_list_voice_state_step_kernel(
@@ -50,58 +51,65 @@ def tile_list_voice_state_step_kernel(
         def keep_tile(shape, dtype, name):
             return held.tile(shape, dtype, name=name, align_bytes=64)
 
-        def bank(name, tag):
+        def bank(name):
             return psum.tile([P, W], F32, name=name, tag="bank", bufs=8)
 
         tab_sc = keep_tile([P, T], U8, "tab_sc")
         wc_sc = keep_tile([P, H], U8, "wc_sc")
         ug_sc = keep_tile([P, H], U8, "ug_sc")
-        nc.gpsimd.memset(ug_sc[:].bitcast(I32), 0)
-        warm = keep_tile([P, 8], F32, "warm")
-        nc.gpsimd.memset(warm[:, 0:1], 0.0)
-        nc.scalar.activation(out=warm[:, 4:5], in_=warm[:, 0:1], func=ACT.Sigmoid)
-
-        ident = keep_tile([P, P], F32, "ident")
-        make_identity(nc, ident[:])
-
+        gain_sb = keep_tile([P, 2, 4], F32, "gain_sb")
+        wgt_sb = keep_tile([P, M], F32, "wgt_sb")
+        wc_raw = keep_tile([P, 2 * H], U8, "wc_raw")
+        ug_raw = keep_tile([P, 2 * H], I32, "ug_raw")
+        tab_raw = raw_tile([P, T], I32, "tab_raw")
         list1 = held.tile([P, S // 16], U16, name="list1")
         list2 = held.tile([P, M // 16], U16, name="list2")
-        nc.sync.dma_start(list1[:], offs)
-        wc_raw = keep_tile([P, 2 * H], U8, "wc_raw")
-        nc.sync.dma_start(out=wc_raw[:].bitcast(I32), in_=wc_words[0].bitcast(I32))
-        for q in range(4):
-            nc.sync.dma_start(out=tab_sc[32 * q : 32 * q + 32, :].bitcast(I32), in_=tab_scales[0, 4 * q : 4 * q + 4, :].bitcast(I32).partition_broadcast(8))
-        pros_rows = pros.rearrange("(p j) c -> p j c", j=4)
-        pros_raw = [keep_tile([P, 4, HALF], F32, f"pros{s}") for s in range(2)]
-        nc.sync.dma_start(out=pros_raw[0][:], in_=pros_rows[:, :, 0:HALF])
-        tab_raw = raw_tile([P, T], I32, "tab_raw")
-        nc.sync.dma_start(out=tab_raw[:], in_=tab_words[0].rearrange("p t i -> p (t i)").bitcast(I32))
-        for q in range(4):
-            nc.sync.dma_start(out=wc_sc[32 * q : 32 * q + 32, :].bitcast(I32), in_=wc_scales[0, 4 * q : 4 * q + 4, :].bitcast(I32).partition_broadcast(8))
-
-        def load_rows(tile, src, a, b):
-            nc.sync.dma_start(out=tile[:], in_=src[W * a : W * (a + 1), W * b : W * (b + 1)].rearrange("(p j) c -> p j c", j=4))
-            return tile
-
-        nc.sync.dma_start(out=pros_raw[1][:], in_=pros_rows[:, :, HALF:M])
-        wgt_sb = keep_tile([P, M], F32, "wgt_sb")
+        warm = keep_tile([P, 8], F32, "warm")
+        nc.gpsimd.memset(warm[:, 0:1], 0.0)
+        nc.gpsimd.memset(ug_sc[:].bitcast(I32), 0)
+        ident = keep_tile([P, P], F32, "ident")
+        make_identity(nc, ident[:])
         raw = {}
-        gain_sb = keep_tile([P, 2, 4], F32, "gain_sb")
         sources = {"st": st, "us": us, "wp": wp, "wo": wo, "pr": pros}
-        for name in LOADS:
-            if name == "wgt":
+        for name in HEAD + LOADS:
+            queue = {"a": nc.scalar, "g": nc.gpsimd, "s": nc.sync}[QUEUE.get(name, "s")]
+            if name == "offs":
+                nc.sync.dma_start(list1[:], offs)
+            elif name == "offs2":
                 nc.sync.dma_start(list2[:], offs2)
-                nc.sync.dma_start(out=wgt_sb[:], in_=wgt)
-            elif name == "ug":
+            elif name == "wc":
+                queue.dma_start(out=wc_raw[:].bitcast(I32), in_=wc_words[0].bitcast(I32))
+            elif name == "tsc":
                 for q in range(4):
-                    nc.sync.dma_start(out=ug_sc[32 * q : 32 * q + 8, :].bitcast(I32), in_=ug_scales[:, 4 * q : 4 * q + 4, :].bitcast(I32))
-                nc.sync.dma_start(out=gain_sb[:], in_=gain.rearrange("(b p t) -> p b t", b=2, t=4))
-                ug_raw = keep_tile([P, 2 * H], I32, "ug_raw")
+                    queue.dma_start(out=tab_sc[32 * q : 32 * q + 32, :].bitcast(I32), in_=tab_scales[0, 4 * q : 4 * q + 4, :].bitcast(I32).partition_broadcast(8))
+            elif name == "wcs":
+                for q in range(4):
+                    queue.dma_start(out=wc_sc[32 * q : 32 * q + 32, :].bitcast(I32), in_=wc_scales[0, 4 * q : 4 * q + 4, :].bitcast(I32).partition_broadcast(8))
+            elif name == "ugs":
+                for q in range(4):
+                    queue.dma_start(out=ug_sc[32 * q : 32 * q + 8, :].bitcast(I32), in_=ug_scales[:, 4 * q : 4 * q + 4, :].bitcast(I32))
+            elif name == "gain":
+                queue.dma_start(out=gain_sb[:], in_=gain.rearrange("(b p t) -> p b t", b=2, t=4))
+            elif name in ("pa", "pb"):
+                s = ("pa", "pb").index(name)
+                raw[name] = keep_tile([P, 4, HALF], F32, name)
+                nc.sync.dma_start(out=raw[name][:], in_=pros.rearrange("(p j) c -> p j c", j=4)[:, :, HALF * s : HALF * (s + 1)])
+            elif name == "wgt":
+                queue.dma_start(out=wgt_sb[:], in_=wgt)
+            elif name == "tab":
+                nc.sync.dma_start(out=tab_raw[:], in_=tab_words[0].rearrange("p t i -> p (t i)").bitcast(I32))
+            elif name == "ug":
                 nc.sync.dma_start(out=ug_raw[:].rearrange("p (a c) -> p a c", a=2), in_=ug_words.rearrange("a p c i -> p a (c i)").bitcast(I32))
             else:
                 make = keep_tile if name[:2] == "st" else raw_tile
-                raw[name] = load_rows(make([P, 4, W], F32, name), sources[name[:2]], int(name[2]), int(name[3]))
+                a, b = int(name[2]), int(name[3])
+                raw[name] = make([P, 4, W], F32, name)
+                nc.sync.dma_start(out=raw[name][:], in_=sources[name[:2]][W * a : W * (a + 1), W * b : W * (b + 1)].rearrange("(p j) c -> p j c", j=4))
+        nc.scalar.activation(out=warm[:, 4:5], in_=warm[:, 0:1], func=ACT.Sigmoid)
         st_raw = [raw["st00"], raw["st10"]]
+
+        def engine_of(name):
+            return "vector" if name in ON_VECTOR else "scalar"
 
         def copy_on(engine, out, in_):
             if engine == "vector":
@@ -109,7 +117,7 @@ def tile_list_voice_state_step_kernel(
             else:
                 nc.scalar.copy(out=out, in_=in_)
 
-        def stage_tile(engine, width, name):
+        def stage_tile(width, name):
             return ring.tile([P, width], BF16, name=name, tag="stage", bufs=STAGE, align_bytes=64)
 
         def weave(engine, out, planes):
@@ -118,18 +126,37 @@ def tile_list_voice_state_step_kernel(
         def deal(engine, out, planes):
             copy_on(engine, out.rearrange("p (t m j) -> p m j t", t=4, j=4), planes.rearrange("p j (m t) -> p m j t", t=4))
 
-        def quantise(rounded, name):
-            width = rounded[:].shape[1] // 4
+        def quantise(rounded, width, name):
             codes = keep_tile([P, width], U32, name + "_codes")
             scales = keep_tile([P, width], U8, name + "_scales")
             nc.vector.quantize_mx(out=codes[:].bitcast(FP8X4), scales=scales[:], in_=rounded[:])
             return codes, scales
 
-        def prepare(layout, names, name):
-            rounded = stage_tile("scalar" if len(names) == 2 else "vector", 4 * W * len(names), name + "_bf")
-            for i, piece in enumerate(names):
-                layout("vector" if piece in ON_VECTOR else "scalar", rounded[:, 4 * W * i : 4 * W * (i + 1)], raw[piece][:])
-            return quantise(rounded, name)
+        def prepare(name):
+            if name == "st":
+                rounded = keep_tile([P, 8 * W], BF16, "st_bf")
+                for a in range(2):
+                    weave(engine_of(f"st{a}0"), rounded[:, 4 * W * a : 4 * W * (a + 1)], raw[f"st{a}0"][:])
+                codes, scales = quantise(rounded, 2 * W, "st")
+                for a in range(2):
+                    made[f"st{a}0"] = (codes[:, W * a : W * (a + 1)], scales[:, W * a : W * (a + 1)])
+                return
+            if name == "pr":
+                rounded = stage_tile(4 * W, "pr_bf")
+                for s, piece in enumerate(("pa", "pb")):
+                    weave(engine_of(piece), rounded[:, 4 * HALF * s : 4 * HALF * (s + 1)], raw[piece][:])
+                made["pr00"] = quantise(rounded, W, "pr")
+                return
+            layout = weave if name[:2] in ("st", "pr", "wp") else deal
+            rounded = stage_tile(4 * W, name + "_bf")
+            layout(engine_of(name), rounded[:], raw[name][:])
+            made[name] = quantise(rounded, W, name)
+
+        def product(acc, lhs, lhs_cols, rhs, rhs_cols, start, stop):
+            nc.tensor.matmul_mx(
+                out=acc, lhsT=lhs[0][:, lhs_cols].bitcast(FP8X4), lhsT_scale=lhs[1][:, lhs_cols],
+                rhs=rhs[0][:, rhs_cols].bitcast(FP8X4), rhs_scale=rhs[1][:, rhs_cols], start=start, stop=stop,
+            )
 
         wc_codes, wc_scd, v_words, v_sc = [], [], [], []
         for s in range(2):
@@ -153,113 +180,102 @@ def tile_list_voice_state_step_kernel(
             v_sc.append(picked)
 
         x = [keep_tile([P, 4, M], F32, f"x{b}") for b in range(2)]
+        made, keep, turned, new_q = {}, {}, {}, {}
+        whole = slice(0, W)
+        y_scales = keep_tile([P, M], U8, "y_scales")
+        y_rows = out_0.rearrange("(p t) m -> p t m", t=4)
+        y_words = out_1[0].rearrange("p m t -> p (m t)").bitcast(I32)
+
         def traits(b):
-            h = [ring.tile([P, S], F32, name=f"h{b}{t}", tag="h", bufs=HBUFS, align_bytes=64) for t in range(4)]
-            for s in range(2):
-                for t in range(4):
-                    acc = bank(f"hacc{b}{t}{s}", "h")
+            for t in range(4):
+                h = ring.tile([P, S], F32, name=f"h{b}{t}", tag="h", bufs=HBUFS, align_bytes=64)
+                for s in range(2):
+                    acc = bank(f"hacc{b}{t}{s}")
                     nc.tensor.matmul_mx(
                         out=acc[:],
                         lhsT=wc_codes[b][:, 2 * P * t : 2 * P * (t + 1)].bitcast(FP4X4), lhsT_scale=wc_scd[b][:, P * t : P * (t + 1)],
                         rhs=v_words[s][:].bitcast(FP8X4), rhs_scale=v_sc[s][:],
                         start=True, stop=True,
                     )
-                    nc.scalar.copy(out=h[t][:, W * s : W * (s + 1)], in_=acc[:])
+                    nc.scalar.copy(out=h[:, W * s : W * (s + 1)], in_=acc[:])
+                nc.vector.tensor_tensor(out=x[b][:, t, :], in0=h[:].indirect(list2[:]), in1=wgt_sb[:], op=MULT)
+
+        def gate(b):
+            for g in range(4):
+                cols = slice(P * g, P * (g + 1))
+                acc = bank(f"z{b}{g}")
+                passes = [(made["pr00"], made[f"wp0{b}"][0][:], made[f"wp0{b}"][1][:])]
+                for a in range(2):
+                    passes.append((made[f"st{a}0"], ug_raw[:, H * a + W * b : H * a + W * (b + 1)], ug_sc[4 * a :, W * b : W * (b + 1)]))
+                passes = passes[Z_LAST:] + passes[:Z_LAST]
+                for i, (lhs, words, scales) in enumerate(passes):
+                    nc.tensor.matmul_mx(
+                        out=acc[:], lhsT=lhs[0][:, cols].bitcast(FP8X4), lhsT_scale=lhs[1][:, cols],
+                        rhs=words.bitcast(FP8X4), rhs_scale=scales, start=(i == 0), stop=(i == 2),
+                    )
+                turned[b, g] = ring.tile([P, 4, P], F32, name=f"turned{b}{g}", tag="turned", bufs=TURNED, align_bytes=64)
+                nc.scalar.activation(out=turned[b, g][:], in_=acc[:].rearrange("m (p t) -> m t p", t=4), func=ACT.Sigmoid)
+
+        def candidate(b):
             for t in range(4):
-                nc.vector.tensor_tensor(out=x[b][:, t, :], in0=h[t][:].indirect(list2[:]), in1=wgt_sb[:], op=MULT)
+                acc = bank(f"u{b}{t}")
+                for a in U_ORDER:
+                    product(acc[:], made[f"us{a}{b}"], slice(P * t, P * (t + 1)), made[f"st{a}0"], whole, a == U_ORDER[0], a == U_ORDER[1])
+                nc.vector.tensor_tensor(out=x[b][:, t, :], in0=acc[:], in1=x[b][:, t, :], op=ADD)
+                nc.scalar.activation(out=x[b][:, t, :], in_=x[b][:, t, :], func=ACT.Tanh)
 
-        def product(acc, lhs, lhs_cols, rhs, rhs_cols, start, stop, lhs_scale=None):
-            nc.tensor.matmul_mx(
-                out=acc, lhsT=lhs[0][:, lhs_cols].bitcast(FP8X4), lhsT_scale=lhs[1][:, lhs_cols] if lhs_scale is None else lhs_scale,
-                rhs=rhs[0][:, rhs_cols].bitcast(FP8X4), rhs_scale=rhs[1][:, rhs_cols], start=start, stop=stop,
-            )
-
-        y_scales = keep_tile([P, M], U8, "y_scales")
-        y_rows = out_0.rearrange("(p t) m -> p t m", t=4)
-        y_words = out_1[0].rearrange("p m t -> p (m t)").bitcast(I32)
-        new_q = {}
+        def fade(b):
+            for t in range(4):
+                acc = bank(f"k{b}{t}")
+                for g in range(4):
+                    nc.tensor.transpose(acc[:, P * g : P * (g + 1)], turned[b, g][:, t, :], ident[:])
+                keep[b, t] = keep_tile([P, M], F32, f"keep{b}{t}")
+                nc.vector.tensor_tensor(out=keep[b, t][:], in0=acc[:], in1=st_raw[b][:, t, :], op=MULT)
 
         def blend(b, s):
-            cols = slice(*CHUNKS[s])
-            wide = cols.stop - cols.start
-            planes = ring.tile([P, 4, wide], BF16, name=f"new{b}{s}", tag="h", bufs=HBUFS, align_bytes=64)
+            cols = slice(HALF * s, HALF * (s + 1))
+            planes = ring.tile([P, 4, HALF], BF16, name=f"new{b}{s}", tag="h", bufs=HBUFS, align_bytes=64)
             for t in range(4):
                 nc.vector.scalar_tensor_tensor(
                     out=planes[:, t, :], in0=x[b][:, t, cols], scalar=gain_sb[:, b, t : t + 1],
                     in1=keep[b, t][:, cols], op0=MULT, op1=ADD,
                 )
-            rounded = stage_tile("scalar", 4 * wide, f"new_bf{b}{s}")
-            weave("vector" if f"n{b}{s}" in ON_VECTOR else "scalar", rounded[:], planes[:])
-            new_q[b, s] = quantise(rounded, f"newq{b}{s}")
+            rounded = stage_tile(4 * HALF, f"new_bf{b}{s}")
+            weave(engine_of(f"n{b}{s}"), rounded[:], planes[:])
+            new_q[b, s] = quantise(rounded, HALF, f"newq{b}{s}")
 
         def finish(s):
-            cols = slice(*CHUNKS[s])
-            wide = cols.stop - cols.start
-            y = ring.tile([P, 4, wide], F32, name=f"y{s}", tag="h", bufs=HBUFS, align_bytes=64)
+            cols = slice(HALF * s, HALF * (s + 1))
+            y = ring.tile([P, 4, HALF], F32, name=f"y{s}", tag="h", bufs=HBUFS, align_bytes=64)
             per = Y_PER_BANK[s]
             for u in range(4 // per):
-                acc = bank(f"y{s}{u}", "h")
+                acc = bank(f"y{s}{u}")
                 for e in range(per):
                     t = per * u + e
                     for b in range(2):
-                        product(acc[:, wide * e : wide * (e + 1)], made[f"wo{b}0"], slice(P * t, P * (t + 1)), new_q[b, s], slice(0, wide), b == 0, b == 1)
-                copy_on("vector" if f"e{s}{u}" in ON_VECTOR else "scalar", y[:, per * u : per * (u + 1), :].rearrange("p e m -> p (e m)"), acc[:, 0 : wide * per])
+                        product(acc[:, HALF * e : HALF * (e + 1)], made[f"wo{b}0"], slice(P * t, P * (t + 1)), new_q[b, s], slice(0, HALF), b == 0, b == 1)
+                copy_on(engine_of(f"e{s}{u}"), y[:, per * u : per * (u + 1), :].rearrange("p e m -> p (e m)"), acc[:, 0 : HALF * per])
             nc.sync.dma_start(out=y_rows[:, :, cols], in_=y[:])
-            rounded = stage_tile("vector", 4 * wide, f"y_bf{s}")
-            weave("vector" if f"y{s}" in ON_VECTOR else "scalar", rounded[:], y[:])
-            y_codes = keep_tile([P, wide], I32, f"y_codes{s}")
+            rounded = stage_tile(4 * HALF, f"y_bf{s}")
+            weave(engine_of(f"y{s}"), rounded[:], y[:])
+            y_codes = keep_tile([P, HALF], I32, f"y_codes{s}")
             nc.vector.quantize_mx(out=y_codes[:].bitcast(FP8X4), scales=y_scales[:, cols], in_=rounded[:])
             nc.sync.dma_start(out=y_words[:, cols], in_=y_codes[:])
 
-        made = {}
-        keep = {}
-        turned = {}
-        whole = slice(0, W)
         for name in PREP:
-            if name == "pr00":
-                rounded = stage_tile("scalar", 4 * W, "pros_bf")
-                for s in range(2):
-                    weave("scalar", rounded[:, 4 * HALF * s : 4 * HALF * (s + 1)], pros_raw[s][:])
-                made[name] = quantise(rounded, name)
-            elif name[0] == "h":
+            if name[0] == "h":
                 traits(int(name[1]))
             elif name[0] == "n":
                 blend(int(name[1]), int(name[2]))
             elif name[0] == "y":
                 finish(int(name[1]))
             elif name[0] == "z":
-                b = int(name[1])
-                for g in range(4):
-                    cols = slice(P * g, P * (g + 1))
-                    acc = bank(f"z{b}{g}", "z")
-                    product(acc[:], made["pr00"], cols, made[f"wp0{b}"], whole, True, False)
-                    for a in range(2):
-                        nc.tensor.matmul_mx(
-                            out=acc[:], lhsT=made[f"st{a}0"][0][:, cols].bitcast(FP8X4), lhsT_scale=made[f"st{a}0"][1][:, cols],
-                            rhs=ug_raw[:, H * a + W * b : H * a + W * (b + 1)].bitcast(FP8X4), rhs_scale=ug_sc[4 * a :, W * b : W * (b + 1)],
-                            start=False, stop=(a == 1),
-                        )
-                    turned[b, g] = ring.tile([P, 4, P], F32, name=f"turned{b}{g}", tag="turned", bufs=TURNED, align_bytes=64)
-                    nc.scalar.activation(out=turned[b, g][:], in_=acc[:].rearrange("m (p t) -> m t p", t=4), func=ACT.Sigmoid)
+                gate(int(name[1]))
             elif name[0] == "c":
-                b = int(name[1])
-                for t in range(4):
-                    cols = slice(W * b + P * t, W * b + P * (t + 1))
-                    acc = bank(f"u{b}{t}", "u")
-                    for a in U_ORDER:
-                        product(acc[:], made[f"us{a}{b}"], slice(P * t, P * (t + 1)), made[f"st{a}0"], whole, a == U_ORDER[0], a == U_ORDER[1])
-                    nc.vector.tensor_tensor(out=x[b][:, t, :], in0=acc[:], in1=x[b][:, t, :], op=ADD)
-                    nc.scalar.activation(out=x[b][:, t, :], in_=x[b][:, t, :], func=ACT.Tanh)
+                candidate(int(name[1]))
             elif name[0] == "A":
-                b = int(name[1])
-                for t in range(4):
-                    acc = bank(f"k{b}{t}", "z")
-                    for g in range(4):
-                        nc.tensor.transpose(acc[:, P * g : P * (g + 1)], turned[b, g][:, t, :], ident[:])
-                    keep[b, t] = keep_tile([P, M], F32, f"keep{b}{t}")
-                    nc.vector.tensor_tensor(out=keep[b, t][:], in0=acc[:], in1=st_raw[b][:, t, :], op=MULT)
+                fade(int(name[1]))
             else:
-                made[name] = prepare(weave if name[:2] in ("st", "pr", "wp") else deal, [name], name)
-
+                prepare(name)
         for q in range(4):
             nc.scalar.dma_start(out=out_2[0, 4 * q : 4 * q + 4, :].bitcast(I32), in_=y_scales[32 * q : 32 * q + 4, :].bitcast(I32))

@@ -3,8 +3,9 @@ from contextlib import ExitStack
 import concourse.mybir as mybir
 from concourse.masks import make_identity
 
-T, S, M, K, H, N = 2048, 1024, 512, 512, 1024, 512
-FLOPS = 2 * (K * H * S + 2 * H * H * M + K * H * M + H * N * M)
+T, S, M = 2048, 1024, 512
+K, F, H, N = 512, 512, 1024, 512
+FLOPS = 2 * (K * H * S + 2 * H * H * M + F * H * M + H * N * M)
 
 F32 = mybir.dt.float32
 BF16 = mybir.dt.bfloat16
@@ -20,19 +21,12 @@ ADD = mybir.AluOpType.add
 
 P = 128
 W = 512
-HALF = 256
-HEAD = ["offs", "wc", "tsc", "offs2", "tab", "st00", "wcs", "st10", "wgt"]
-LOADS = ["pr00", "wp00", "ug", "ugs", "wp01", "us00", "us10", "us01", "us11", "gain", "wo00", "wo10"]
-PREP = ["st", "h0", "pr00", "wp00", "h1", "wp01", "us00", "z0", "us10", "us01", "z1", "A0", "us11", "c0", "wo00", "A1", "wo10", "c1", "n00", "n10", "n01", "y0", "n11", "y1"]
-ON_VECTOR = ["st10", "wp00", "us10", "us11", "n11", "e11", "e13", "y1", "y0"]
-QUEUE = {}
-U_ORDER = (0, 1)
-Z_LAST = 1
-RAWBUFS = 7
-STAGE = 6
-HBUFS = 7
-TURNED = 4
-Y_PER_BANK = [1, 1]
+HALF = M // 2
+LIST_COLS = W // 16
+RAW_BUFS = 7
+ROUNDED_BUFS = 6
+SCRATCH_BUFS = 7
+GATE_BUFS = 4
 
 
 def tile_list_voice_state_step_kernel(
@@ -45,237 +39,220 @@ def tile_list_voice_state_step_kernel(
         ring = ctx.enter_context(tc.tile_pool(name="ring", bufs=1))
         psum = ctx.enter_context(tc.psum_pool(name="psum", bufs=1))
 
-        def raw_tile(shape, dtype, name):
-            return ring.tile(shape, dtype, name=name, tag="raw", bufs=RAWBUFS, align_bytes=64)
-
-        def keep_tile(shape, dtype, name):
+        def held_tile(shape, dtype, name):
             return held.tile(shape, dtype, name=name, align_bytes=64)
+
+        def raw_tile(shape, dtype, name):
+            return ring.tile(shape, dtype, name=name, tag="raw", bufs=RAW_BUFS, align_bytes=64)
+
+        def rounded_tile(width, name):
+            return ring.tile([P, width], BF16, name=name, tag="rounded", bufs=ROUNDED_BUFS, align_bytes=64)
+
+        def scratch_tile(shape, dtype, name):
+            return ring.tile(shape, dtype, name=name, tag="scratch", bufs=SCRATCH_BUFS, align_bytes=64)
 
         def bank(name):
             return psum.tile([P, W], F32, name=name, tag="bank", bufs=8)
 
-        tab_sc = keep_tile([P, T], U8, "tab_sc")
-        wc_sc = keep_tile([P, H], U8, "wc_sc")
-        ug_sc = keep_tile([P, H], U8, "ug_sc")
-        gain_sb = keep_tile([P, 2, 4], F32, "gain_sb")
-        wgt_sb = keep_tile([P, M], F32, "wgt_sb")
-        wc_raw = keep_tile([P, 2 * H], U8, "wc_raw")
-        ug_raw = keep_tile([P, 2 * H], I32, "ug_raw")
+        def load_pass(make, src, a, b, name):
+            tile = make([P, 4, W], F32, name)
+            nc.sync.dma_start(out=tile[:], in_=src[W * a : W * (a + 1), W * b : W * (b + 1)].rearrange("(p j) c -> p j c", j=4))
+            return tile
+
+        def load_scale_rows(tile, src):
+            for q in range(4):
+                rows = src[0, 4 * q : 4 * q + 4, :].bitcast(I32)
+                nc.sync.dma_start(out=tile[32 * q : 32 * (q + 1), :].bitcast(I32), in_=rows.partition_broadcast(8))
+
+        tab_sc = held_tile([P, T], U8, "tab_sc")
+        wc_sc = held_tile([P, H], U8, "wc_sc")
+        ug_sc = held_tile([P, H], U8, "ug_sc")
+        gain_sb = held_tile([P, 2, 4], F32, "gain_sb")
+        wgt_sb = held_tile([P, M], F32, "wgt_sb")
+        wc_raw = held_tile([P, 2 * H], U8, "wc_raw")
+        ug_raw = held_tile([P, 2 * H], I32, "ug_raw")
         tab_raw = raw_tile([P, T], I32, "tab_raw")
-        list1 = held.tile([P, S // 16], U16, name="list1")
-        list2 = held.tile([P, M // 16], U16, name="list2")
-        warm = keep_tile([P, 8], F32, "warm")
+        frames = held.tile([P, S // 16], U16, name="frames")
+        picks = held.tile([P, M // 16], U16, name="picks")
+        warm = held_tile([P, 8], F32, "warm")
         nc.gpsimd.memset(warm[:, 0:1], 0.0)
         nc.gpsimd.memset(ug_sc[:].bitcast(I32), 0)
-        ident = keep_tile([P, P], F32, "ident")
+        ident = held_tile([P, P], F32, "ident")
         make_identity(nc, ident[:])
-        raw = {}
-        sources = {"st": st, "us": us, "wp": wp, "wo": wo, "pr": pros}
-        for name in HEAD + LOADS:
-            queue = {"a": nc.scalar, "g": nc.gpsimd, "s": nc.sync}[QUEUE.get(name, "s")]
-            if name == "offs":
-                nc.sync.dma_start(list1[:], offs)
-            elif name == "offs2":
-                nc.sync.dma_start(list2[:], offs2)
-            elif name == "wc":
-                queue.dma_start(out=wc_raw[:].bitcast(I32), in_=wc_words[0].bitcast(I32))
-            elif name == "tsc":
-                for q in range(4):
-                    queue.dma_start(out=tab_sc[32 * q : 32 * q + 32, :].bitcast(I32), in_=tab_scales[0, 4 * q : 4 * q + 4, :].bitcast(I32).partition_broadcast(8))
-            elif name == "wcs":
-                for q in range(4):
-                    queue.dma_start(out=wc_sc[32 * q : 32 * q + 32, :].bitcast(I32), in_=wc_scales[0, 4 * q : 4 * q + 4, :].bitcast(I32).partition_broadcast(8))
-            elif name == "ugs":
-                for q in range(4):
-                    queue.dma_start(out=ug_sc[32 * q : 32 * q + 8, :].bitcast(I32), in_=ug_scales[:, 4 * q : 4 * q + 4, :].bitcast(I32))
-            elif name == "gain":
-                queue.dma_start(out=gain_sb[:], in_=gain.rearrange("(b p t) -> p b t", b=2, t=4))
-            elif name in ("pa", "pb"):
-                s = ("pa", "pb").index(name)
-                raw[name] = keep_tile([P, 4, HALF], F32, name)
-                nc.sync.dma_start(out=raw[name][:], in_=pros.rearrange("(p j) c -> p j c", j=4)[:, :, HALF * s : HALF * (s + 1)])
-            elif name == "wgt":
-                queue.dma_start(out=wgt_sb[:], in_=wgt)
-            elif name == "tab":
-                nc.sync.dma_start(out=tab_raw[:], in_=tab_words[0].rearrange("p t i -> p (t i)").bitcast(I32))
-            elif name == "ug":
-                nc.sync.dma_start(out=ug_raw[:].rearrange("p (a c) -> p a c", a=2), in_=ug_words.rearrange("a p c i -> p a (c i)").bitcast(I32))
-            else:
-                make = keep_tile if name[:2] == "st" else raw_tile
-                a, b = int(name[2]), int(name[3])
-                raw[name] = make([P, 4, W], F32, name)
-                nc.sync.dma_start(out=raw[name][:], in_=sources[name[:2]][W * a : W * (a + 1), W * b : W * (b + 1)].rearrange("(p j) c -> p j c", j=4))
+
+        nc.sync.dma_start(frames[:], offs)
+        nc.sync.dma_start(out=wc_raw[:].bitcast(I32), in_=wc_words[0].bitcast(I32))
+        load_scale_rows(tab_sc, tab_scales)
+        nc.sync.dma_start(picks[:], offs2)
+        nc.sync.dma_start(out=tab_raw[:], in_=tab_words[0].rearrange("p t i -> p (t i)").bitcast(I32))
+        st_raw = [load_pass(held_tile, st, 0, 0, "st0")]
+        load_scale_rows(wc_sc, wc_scales)
+        st_raw.append(load_pass(held_tile, st, 1, 0, "st1"))
+        nc.sync.dma_start(out=wgt_sb[:], in_=wgt)
+        pros_raw = load_pass(raw_tile, pros, 0, 0, "pros")
+        wp_raw = [load_pass(raw_tile, wp, 0, 0, "wp0")]
+        nc.sync.dma_start(
+            out=ug_raw[:].rearrange("p (a c) -> p a c", a=2), in_=ug_words.rearrange("a p c i -> p a (c i)").bitcast(I32)
+        )
+        for q in range(4):
+            nc.sync.dma_start(
+                out=ug_sc[32 * q : 32 * q + 8, :].bitcast(I32), in_=ug_scales[:, 4 * q : 4 * q + 4, :].bitcast(I32)
+            )
+        wp_raw.append(load_pass(raw_tile, wp, 0, 1, "wp1"))
+        us_raw = [[load_pass(raw_tile, us, a, b, f"us{a}{b}") for a in range(2)] for b in range(2)]
+        nc.sync.dma_start(out=gain_sb[:], in_=gain.rearrange("(b p t) -> p b t", b=2, t=4))
+        wo_raw = [load_pass(raw_tile, wo, b, 0, f"wo{b}") for b in range(2)]
+
         nc.scalar.activation(out=warm[:, 4:5], in_=warm[:, 0:1], func=ACT.Sigmoid)
-        st_raw = [raw["st00"], raw["st10"]]
 
-        def engine_of(name):
-            return "vector" if name in ON_VECTOR else "scalar"
+        on_vector, on_scalar = nc.vector.tensor_copy, nc.scalar.copy
 
-        def copy_on(engine, out, in_):
-            if engine == "vector":
-                nc.vector.tensor_copy(out=out, in_=in_)
-            else:
-                nc.scalar.copy(out=out, in_=in_)
+        def weave(copy, out, planes):
+            copy(out=out.rearrange("p (c i j) -> p c j i", i=4, j=4), in_=planes.rearrange("p j (c i) -> p c j i", i=4))
 
-        def stage_tile(width, name):
-            return ring.tile([P, width], BF16, name=name, tag="stage", bufs=STAGE, align_bytes=64)
-
-        def weave(engine, out, planes):
-            copy_on(engine, out.rearrange("p (c i j) -> p c j i", i=4, j=4), planes.rearrange("p j (c i) -> p c j i", i=4))
-
-        def deal(engine, out, planes):
-            copy_on(engine, out.rearrange("p (t m j) -> p m j t", t=4, j=4), planes.rearrange("p j (m t) -> p m j t", t=4))
+        def weave_and_deal(copy, out, planes):
+            for u in range(2):
+                copy(
+                    out=out.rearrange("p (u e m j) -> p u m j e", u=2, e=2, j=4)[:, u],
+                    in_=planes.rearrange("p j (m u e) -> p u m j e", u=2, e=2)[:, u],
+                )
 
         def quantise(rounded, width, name):
-            codes = keep_tile([P, width], U32, name + "_codes")
-            scales = keep_tile([P, width], U8, name + "_scales")
+            codes = held_tile([P, width], U32, name + "_codes")
+            scales = held_tile([P, width], U8, name + "_scales")
             nc.vector.quantize_mx(out=codes[:].bitcast(FP8X4), scales=scales[:], in_=rounded[:])
             return codes, scales
 
-        def prepare(name):
-            if name == "st":
-                rounded = keep_tile([P, 8 * W], BF16, "st_bf")
-                for a in range(2):
-                    weave(engine_of(f"st{a}0"), rounded[:, 4 * W * a : 4 * W * (a + 1)], raw[f"st{a}0"][:])
-                codes, scales = quantise(rounded, 2 * W, "st")
-                for a in range(2):
-                    made[f"st{a}0"] = (codes[:, W * a : W * (a + 1)], scales[:, W * a : W * (a + 1)])
-                return
-            if name == "pr":
-                rounded = stage_tile(4 * W, "pr_bf")
-                for s, piece in enumerate(("pa", "pb")):
-                    weave(engine_of(piece), rounded[:, 4 * HALF * s : 4 * HALF * (s + 1)], raw[piece][:])
-                made["pr00"] = quantise(rounded, W, "pr")
-                return
-            layout = weave if name[:2] in ("st", "pr", "wp") else deal
-            rounded = stage_tile(4 * W, name + "_bf")
-            layout(engine_of(name), rounded[:], raw[name][:])
-            made[name] = quantise(rounded, W, name)
+        def prepare(layout, copy, planes, name):
+            rounded = rounded_tile(4 * W, name + "_bf")
+            layout(copy, rounded[:], planes[:])
+            return quantise(rounded, W, name)
 
-        def product(acc, lhs, lhs_cols, rhs, rhs_cols, start, stop):
+        def product(acc, lhs, rhs, start, stop):
             nc.tensor.matmul_mx(
-                out=acc, lhsT=lhs[0][:, lhs_cols].bitcast(FP8X4), lhsT_scale=lhs[1][:, lhs_cols],
-                rhs=rhs[0][:, rhs_cols].bitcast(FP8X4), rhs_scale=rhs[1][:, rhs_cols], start=start, stop=stop,
+                out=acc, lhsT=lhs[0].bitcast(FP8X4), lhsT_scale=lhs[1], rhs=rhs[0].bitcast(FP8X4), rhs_scale=rhs[1],
+                start=start, stop=stop,
             )
 
-        wc_codes, wc_scd, v_words, v_sc = [], [], [], []
+        def columns(operand, first, count):
+            return operand[0][:, first : first + count], operand[1][:, first : first + count]
+
+        wc_q, v_q = [], []
         for s in range(2):
-            codes = keep_tile([P, 2 * W], U8, f"wc_codes{s}")
+            codes = held_tile([P, 2 * W], U8, f"wc_codes{s}")
             nc.vector.tensor_copy(
-                out=codes[:].rearrange("p (t m e) -> p t m e", t=4, e=2),
-                in_=wc_raw[:, 2 * W * s : 2 * W * (s + 1)].rearrange("p (m t e) -> p t m e", t=4, e=2),
+                out=codes[:].bitcast(U16).rearrange("p (t m) -> p t m", t=4),
+                in_=wc_raw[:, 2 * W * s : 2 * W * (s + 1)].bitcast(U16).rearrange("p (m t) -> p t m", t=4),
             )
-            wc_codes.append(codes)
-            scales = keep_tile([P, W], U8, f"wc_scd{s}")
+            scales = held_tile([P, W], U8, f"wc_scales{s}")
             nc.vector.tensor_copy(
                 out=scales[:].rearrange("p (t m) -> p t m", t=4),
                 in_=wc_sc[:, W * s : W * (s + 1)].rearrange("p (m t) -> p t m", t=4),
             )
-            wc_scd.append(scales)
-            picked = keep_tile([P, W], U32, f"v_words{s}")
-            nc.vector.tensor_copy(out=picked[:], in_=tab_raw[:].bitcast(U32).indirect(list1[:, 32 * s : 32 * (s + 1)]))
-            v_words.append(picked)
-            picked = keep_tile([P, W], U8, f"v_sc{s}")
-            nc.vector.tensor_copy(out=picked[:], in_=tab_sc[:].indirect(list1[:, 32 * s : 32 * (s + 1)]))
-            v_sc.append(picked)
+            wc_q.append((codes, scales))
+            part = frames[:, LIST_COLS * s : LIST_COLS * (s + 1)]
+            words = held_tile([P, W], U32, f"v_words{s}")
+            nc.vector.tensor_copy(out=words[:], in_=tab_raw[:].bitcast(U32).indirect(part))
+            scales = held_tile([P, W], U8, f"v_scales{s}")
+            nc.vector.tensor_copy(out=scales[:], in_=tab_sc[:].indirect(part))
+            v_q.append((words, scales))
 
-        x = [keep_tile([P, 4, M], F32, f"x{b}") for b in range(2)]
-        made, keep, turned, new_q = {}, {}, {}, {}
-        whole = slice(0, W)
-        y_scales = keep_tile([P, M], U8, "y_scales")
-        y_rows = out_0.rearrange("(p t) m -> p t m", t=4)
-        y_words = out_1[0].rearrange("p m t -> p (m t)").bitcast(I32)
+        st_bf = held_tile([P, 8 * W], BF16, "st_bf")
+        for a, copy in enumerate((on_scalar, on_vector)):
+            weave(copy, st_bf[:, 4 * W * a : 4 * W * (a + 1)], st_raw[a][:])
+        st_both = quantise(st_bf, 2 * W, "st")
+        st_q = [columns(st_both, W * a, W) for a in range(2)]
+        pros_q = prepare(weave, on_scalar, pros_raw, "pros")
+        wp_q = [prepare(weave, copy, wp_raw[b], f"wp{b}") for b, copy in enumerate((on_vector, on_scalar))]
+        us_q = [
+            [prepare(weave_and_deal, copy, us_raw[b][a], f"us{a}{b}") for a, copy in enumerate((on_scalar, on_vector))]
+            for b in range(2)
+        ]
+        wo_q = [prepare(weave_and_deal, on_scalar, wo_raw[b], f"wo{b}") for b in range(2)]
 
-        def traits(b):
+        cand = [held_tile([P, 4, M], F32, f"cand{b}") for b in range(2)]
+        for b in range(2):
             for t in range(4):
-                h = ring.tile([P, S], F32, name=f"h{b}{t}", tag="h", bufs=HBUFS, align_bytes=64)
+                h = scratch_tile([P, S], F32, f"h{b}{t}")
                 for s in range(2):
-                    acc = bank(f"hacc{b}{t}{s}")
+                    acc = bank(f"h_acc{b}{t}{s}")
                     nc.tensor.matmul_mx(
                         out=acc[:],
-                        lhsT=wc_codes[b][:, 2 * P * t : 2 * P * (t + 1)].bitcast(FP4X4), lhsT_scale=wc_scd[b][:, P * t : P * (t + 1)],
-                        rhs=v_words[s][:].bitcast(FP8X4), rhs_scale=v_sc[s][:],
-                        start=True, stop=True,
+                        lhsT=wc_q[b][0][:, 2 * P * t : 2 * P * (t + 1)].bitcast(FP4X4),
+                        lhsT_scale=wc_q[b][1][:, P * t : P * (t + 1)],
+                        rhs=v_q[s][0][:].bitcast(FP8X4),
+                        rhs_scale=v_q[s][1][:],
+                        start=True,
+                        stop=True,
                     )
                     nc.scalar.copy(out=h[:, W * s : W * (s + 1)], in_=acc[:])
-                nc.vector.tensor_tensor(out=x[b][:, t, :], in0=h[:].indirect(list2[:]), in1=wgt_sb[:], op=MULT)
+                nc.vector.tensor_tensor(out=cand[b][:, t, :], in0=h[:].indirect(picks[:]), in1=wgt_sb[:], op=MULT)
 
-        def gate(b):
+        gate = {}
+        for b in range(2):
             for g in range(4):
-                cols = slice(P * g, P * (g + 1))
-                acc = bank(f"z{b}{g}")
-                passes = [(made["pr00"], made[f"wp0{b}"][0][:], made[f"wp0{b}"][1][:])]
+                acc = bank(f"gate_acc{b}{g}")
                 for a in range(2):
-                    passes.append((made[f"st{a}0"], ug_raw[:, H * a + W * b : H * a + W * (b + 1)], ug_sc[4 * a :, W * b : W * (b + 1)]))
-                passes = passes[Z_LAST:] + passes[:Z_LAST]
-                for i, (lhs, words, scales) in enumerate(passes):
-                    nc.tensor.matmul_mx(
-                        out=acc[:], lhsT=lhs[0][:, cols].bitcast(FP8X4), lhsT_scale=lhs[1][:, cols],
-                        rhs=words.bitcast(FP8X4), rhs_scale=scales, start=(i == 0), stop=(i == 2),
-                    )
-                turned[b, g] = ring.tile([P, 4, P], F32, name=f"turned{b}{g}", tag="turned", bufs=TURNED, align_bytes=64)
-                nc.scalar.activation(out=turned[b, g][:], in_=acc[:].rearrange("m (p t) -> m t p", t=4), func=ACT.Sigmoid)
+                    ug_pass = ug_raw[:, H * a + W * b : H * a + W * (b + 1)], ug_sc[4 * a :, W * b : W * (b + 1)]
+                    product(acc[:], columns(st_q[a], P * g, P), ug_pass, a == 0, False)
+                product(acc[:], columns(pros_q, P * g, P), columns(wp_q[b], 0, W), False, True)
+                gate[b, g] = ring.tile([P, 4, P], F32, name=f"gate{b}{g}", tag="gate", bufs=GATE_BUFS, align_bytes=64)
+                nc.scalar.activation(out=gate[b, g][:], in_=acc[:].rearrange("m (p t) -> m t p", t=4), func=ACT.Sigmoid)
 
-        def candidate(b):
+        faded = {}
+        for b in range(2):
             for t in range(4):
-                acc = bank(f"u{b}{t}")
-                for a in U_ORDER:
-                    product(acc[:], made[f"us{a}{b}"], slice(P * t, P * (t + 1)), made[f"st{a}0"], whole, a == U_ORDER[0], a == U_ORDER[1])
-                nc.vector.tensor_tensor(out=x[b][:, t, :], in0=acc[:], in1=x[b][:, t, :], op=ADD)
-                nc.scalar.activation(out=x[b][:, t, :], in_=x[b][:, t, :], func=ACT.Tanh)
-
-        def fade(b):
-            for t in range(4):
-                acc = bank(f"k{b}{t}")
+                acc = bank(f"keep{b}{t}")
                 for g in range(4):
-                    nc.tensor.transpose(acc[:, P * g : P * (g + 1)], turned[b, g][:, t, :], ident[:])
-                keep[b, t] = keep_tile([P, M], F32, f"keep{b}{t}")
-                nc.vector.tensor_tensor(out=keep[b, t][:], in0=acc[:], in1=st_raw[b][:, t, :], op=MULT)
+                    nc.tensor.transpose(acc[:, P * g : P * (g + 1)], gate[b, g][:, t, :], ident[:])
+                faded[b, t] = held_tile([P, M], F32, f"faded{b}{t}")
+                nc.vector.tensor_tensor(out=faded[b, t][:], in0=acc[:], in1=st_raw[b][:, t, :], op=MULT)
+            for t in range(4):
+                acc = bank(f"cand_acc{b}{t}")
+                for a in range(2):
+                    product(acc[:], columns(us_q[b][a], P * t, P), st_q[a], a == 0, a == 1)
+                nc.vector.tensor_tensor(out=cand[b][:, t, :], in0=acc[:], in1=cand[b][:, t, :], op=ADD)
+                nc.scalar.activation(out=cand[b][:, t, :], in_=cand[b][:, t, :], func=ACT.Tanh)
 
-        def blend(b, s):
+        y_scales = held_tile([P, M], U8, "y_scales")
+        y_rows = out_0.rearrange("(p t) m -> p t m", t=4)
+        y_words = out_1[0].rearrange("p m t -> p (m t)").bitcast(I32)
+        new_q = {}
+
+        def blend(b, s, copy):
             cols = slice(HALF * s, HALF * (s + 1))
-            planes = ring.tile([P, 4, HALF], BF16, name=f"new{b}{s}", tag="h", bufs=HBUFS, align_bytes=64)
+            planes = scratch_tile([P, 4, HALF], BF16, f"new{b}{s}")
             for t in range(4):
                 nc.vector.scalar_tensor_tensor(
-                    out=planes[:, t, :], in0=x[b][:, t, cols], scalar=gain_sb[:, b, t : t + 1],
-                    in1=keep[b, t][:, cols], op0=MULT, op1=ADD,
+                    out=planes[:, t, :], in0=cand[b][:, t, cols], scalar=gain_sb[:, b, t : t + 1],
+                    in1=faded[b, t][:, cols], op0=MULT, op1=ADD,
                 )
-            rounded = stage_tile(4 * HALF, f"new_bf{b}{s}")
-            weave(engine_of(f"n{b}{s}"), rounded[:], planes[:])
-            new_q[b, s] = quantise(rounded, HALF, f"newq{b}{s}")
+            woven = rounded_tile(4 * HALF, f"new_bf{b}{s}")
+            weave(copy, woven[:], planes[:])
+            new_q[b, s] = quantise(woven, HALF, f"new{b}{s}")
 
-        def finish(s):
+        def finish(s, plane_copies, rounding_copy):
             cols = slice(HALF * s, HALF * (s + 1))
-            y = ring.tile([P, 4, HALF], F32, name=f"y{s}", tag="h", bufs=HBUFS, align_bytes=64)
-            per = Y_PER_BANK[s]
-            for u in range(4 // per):
-                acc = bank(f"y{s}{u}")
-                for e in range(per):
-                    t = per * u + e
-                    for b in range(2):
-                        product(acc[:, HALF * e : HALF * (e + 1)], made[f"wo{b}0"], slice(P * t, P * (t + 1)), new_q[b, s], slice(0, HALF), b == 0, b == 1)
-                copy_on(engine_of(f"e{s}{u}"), y[:, per * u : per * (u + 1), :].rearrange("p e m -> p (e m)"), acc[:, 0 : HALF * per])
+            y = scratch_tile([P, 4, HALF], F32, f"y{s}")
+            for t, copy in enumerate(plane_copies):
+                acc = bank(f"y_acc{s}{t}")
+                for b in range(2):
+                    product(acc[:, 0:HALF], columns(wo_q[b], P * t, P), columns(new_q[b, s], 0, HALF), b == 0, b == 1)
+                copy(out=y[:, t, :], in_=acc[:, 0:HALF])
             nc.sync.dma_start(out=y_rows[:, :, cols], in_=y[:])
-            rounded = stage_tile(4 * HALF, f"y_bf{s}")
-            weave(engine_of(f"y{s}"), rounded[:], y[:])
-            y_codes = keep_tile([P, HALF], I32, f"y_codes{s}")
+            rounded = rounded_tile(4 * HALF, f"y_bf{s}")
+            weave(rounding_copy, rounded[:], y[:])
+            y_codes = held_tile([P, HALF], I32, f"y_codes{s}")
             nc.vector.quantize_mx(out=y_codes[:].bitcast(FP8X4), scales=y_scales[:, cols], in_=rounded[:])
             nc.sync.dma_start(out=y_words[:, cols], in_=y_codes[:])
 
-        for name in PREP:
-            if name[0] == "h":
-                traits(int(name[1]))
-            elif name[0] == "n":
-                blend(int(name[1]), int(name[2]))
-            elif name[0] == "y":
-                finish(int(name[1]))
-            elif name[0] == "z":
-                gate(int(name[1]))
-            elif name[0] == "c":
-                candidate(int(name[1]))
-            elif name[0] == "A":
-                fade(int(name[1]))
-            else:
-                prepare(name)
+        blend(0, 0, on_scalar)
+        blend(1, 0, on_scalar)
+        blend(0, 1, on_scalar)
+        finish(0, (on_scalar,) * 4, on_scalar)
+        blend(1, 1, on_vector)
+        finish(1, (on_scalar, on_vector) * 2, on_vector)
         for q in range(4):
-            nc.scalar.dma_start(out=out_2[0, 4 * q : 4 * q + 4, :].bitcast(I32), in_=y_scales[32 * q : 32 * q + 4, :].bitcast(I32))
+            nc.scalar.dma_start(
+                out=out_2[0, 4 * q : 4 * q + 4, :].bitcast(I32), in_=y_scales[32 * q : 32 * q + 4, :].bitcast(I32)
+            )

@@ -61,8 +61,7 @@ def tile_list_voice_state_step_kernel(
 
         def load_scale_rows(tile, src):
             for q in range(4):
-                rows = src[0, 4 * q : 4 * q + 4, :].bitcast(I32)
-                nc.sync.dma_start(out=tile[32 * q : 32 * (q + 1), :].bitcast(I32), in_=rows.partition_broadcast(8))
+                nc.sync.dma_start(out=tile[32 * q : 32 * q + 4, :].bitcast(I32), in_=src[0, 4 * q : 4 * q + 4, :].bitcast(I32))
 
         tab_sc = held_tile([P, T], U8, "tab_sc")
         wc_sc = held_tile([P, H], U8, "wc_sc")
@@ -74,16 +73,15 @@ def tile_list_voice_state_step_kernel(
         tab_raw = raw_tile([P, T], I32, "tab_raw")
         frames = held.tile([P, S // 16], U16, name="frames")
         picks = held.tile([P, M // 16], U16, name="picks")
-        warm = held_tile([P, 8], F32, "warm")
-        nc.gpsimd.memset(warm[:, 0:1], 0.0)
-        nc.gpsimd.memset(ug_sc[:].bitcast(I32), 0)
+        for scale_tile in (tab_sc, wc_sc, ug_sc):
+            nc.gpsimd.memset(scale_tile[:].bitcast(I32), 0)
         ident = held_tile([P, P], F32, "ident")
         make_identity(nc, ident[:])
 
         nc.sync.dma_start(frames[:], offs)
         nc.sync.dma_start(out=wc_raw[:].bitcast(I32), in_=wc_words[0].bitcast(I32))
-        load_scale_rows(tab_sc, tab_scales)
         nc.sync.dma_start(picks[:], offs2)
+        load_scale_rows(tab_sc, tab_scales)
         nc.sync.dma_start(out=tab_raw[:], in_=tab_words[0].rearrange("p t i -> p (t i)").bitcast(I32))
         st_raw = [load_pass(held_tile, st, 0, 0, "st0")]
         load_scale_rows(wc_sc, wc_scales)
@@ -103,19 +101,16 @@ def tile_list_voice_state_step_kernel(
         nc.sync.dma_start(out=gain_sb[:], in_=gain.rearrange("(b p t) -> p b t", b=2, t=4))
         wo_raw = [load_pass(raw_tile, wo, b, 0, f"wo{b}") for b in range(2)]
 
-        nc.scalar.activation(out=warm[:, 4:5], in_=warm[:, 0:1], func=ACT.Sigmoid)
-
         on_vector, on_scalar = nc.vector.tensor_copy, nc.scalar.copy
+
+        def halved_on_scalar(out, in_):
+            nc.scalar.activation(out=out, in_=in_, func=ACT.Copy, scale=0.5)
 
         def weave(copy, out, planes):
             copy(out=out.rearrange("p (c i j) -> p c j i", i=4, j=4), in_=planes.rearrange("p j (c i) -> p c j i", i=4))
 
         def weave_and_deal(copy, out, planes):
-            for u in range(2):
-                copy(
-                    out=out.rearrange("p (u e m j) -> p u m j e", u=2, e=2, j=4)[:, u],
-                    in_=planes.rearrange("p j (m u e) -> p u m j e", u=2, e=2)[:, u],
-                )
+            copy(out=out.rearrange("p (t m j) -> p m j t", t=4, j=4), in_=planes.rearrange("p j (m t) -> p m j t", t=4))
 
         def quantise(rounded, width, name):
             codes = held_tile([P, width], U32, name + "_codes")
@@ -137,25 +132,31 @@ def tile_list_voice_state_step_kernel(
         def columns(operand, first, count):
             return operand[0][:, first : first + count], operand[1][:, first : first + count]
 
-        wc_q, v_q = [], []
-        for s in range(2):
-            codes = held_tile([P, 2 * W], U8, f"wc_codes{s}")
+        def deal_wc(b):
+            codes = held_tile([P, 2 * W], U8, f"wc_codes{b}")
             nc.vector.tensor_copy(
                 out=codes[:].bitcast(U16).rearrange("p (t m) -> p t m", t=4),
-                in_=wc_raw[:, 2 * W * s : 2 * W * (s + 1)].bitcast(U16).rearrange("p (m t) -> p t m", t=4),
+                in_=wc_raw[:, 2 * W * b : 2 * W * (b + 1)].bitcast(U16).rearrange("p (m t) -> p t m", t=4),
             )
-            scales = held_tile([P, W], U8, f"wc_scales{s}")
+            scales = held_tile([P, W], U8, f"wc_scales{b}")
             nc.vector.tensor_copy(
                 out=scales[:].rearrange("p (t m) -> p t m", t=4),
-                in_=wc_sc[:, W * s : W * (s + 1)].rearrange("p (m t) -> p t m", t=4),
+                in_=wc_sc[:, W * b : W * (b + 1)].rearrange("p (m t) -> p t m", t=4),
             )
-            wc_q.append((codes, scales))
-            part = frames[:, LIST_COLS * s : LIST_COLS * (s + 1)]
-            words = held_tile([P, W], U32, f"v_words{s}")
-            nc.vector.tensor_copy(out=words[:], in_=tab_raw[:].bitcast(U32).indirect(part))
-            scales = held_tile([P, W], U8, f"v_scales{s}")
-            nc.vector.tensor_copy(out=scales[:], in_=tab_sc[:].indirect(part))
-            v_q.append((words, scales))
+            return codes, scales
+
+        def gather_frames(f):
+            offsets = frames[:, LIST_COLS * f : LIST_COLS * (f + 1)]
+            codes = held_tile([P, W], U32, f"v_codes{f}")
+            nc.vector.tensor_copy(out=codes[:], in_=tab_raw[:].bitcast(U32).indirect(offsets))
+            scales = held_tile([P, W], U8, f"v_scales{f}")
+            nc.vector.tensor_copy(out=scales[:], in_=tab_sc[:].indirect(offsets))
+            return codes, scales
+
+        wc_q, v_q = [], []
+        for i in range(2):
+            wc_q.append(deal_wc(i))
+            v_q.append(gather_frames(i))
 
         st_bf = held_tile([P, 8 * W], BF16, "st_bf")
         for a, copy in enumerate((on_scalar, on_vector)):
@@ -168,45 +169,49 @@ def tile_list_voice_state_step_kernel(
             [prepare(weave_and_deal, copy, us_raw[b][a], f"us{a}{b}") for a, copy in enumerate((on_scalar, on_vector))]
             for b in range(2)
         ]
-        wo_q = [prepare(weave_and_deal, on_scalar, wo_raw[b], f"wo{b}") for b in range(2)]
+        wo_q = [prepare(weave_and_deal, halved_on_scalar, wo_raw[b], f"wo{b}") for b in range(2)]
+        gain2 = held_tile([P, 2, 4], F32, "gain2")
+        nc.scalar.activation(out=gain2[:], in_=gain_sb[:], func=ACT.Copy, scale=2.0)
 
         cand = [held_tile([P, 4, M], F32, f"cand{b}") for b in range(2)]
         for b in range(2):
             for t in range(4):
                 h = scratch_tile([P, S], F32, f"h{b}{t}")
-                for s in range(2):
-                    acc = bank(f"h_acc{b}{t}{s}")
+                for f in range(2):
+                    acc = bank(f"h_acc{b}{t}{f}")
                     nc.tensor.matmul_mx(
                         out=acc[:],
                         lhsT=wc_q[b][0][:, 2 * P * t : 2 * P * (t + 1)].bitcast(FP4X4),
                         lhsT_scale=wc_q[b][1][:, P * t : P * (t + 1)],
-                        rhs=v_q[s][0][:].bitcast(FP8X4),
-                        rhs_scale=v_q[s][1][:],
+                        rhs=v_q[f][0][:].bitcast(FP8X4),
+                        rhs_scale=v_q[f][1][:],
                         start=True,
                         stop=True,
                     )
-                    nc.scalar.copy(out=h[:, W * s : W * (s + 1)], in_=acc[:])
+                    nc.scalar.copy(out=h[:, W * f : W * (f + 1)], in_=acc[:])
                 nc.vector.tensor_tensor(out=cand[b][:, t, :], in0=h[:].indirect(picks[:]), in1=wgt_sb[:], op=MULT)
 
         gate = {}
         for b in range(2):
-            for g in range(4):
-                acc = bank(f"gate_acc{b}{g}")
+            for blk in range(4):
+                acc = bank(f"gate_acc{b}{blk}")
                 for a in range(2):
                     ug_pass = ug_raw[:, H * a + W * b : H * a + W * (b + 1)], ug_sc[4 * a :, W * b : W * (b + 1)]
-                    product(acc[:], columns(st_q[a], P * g, P), ug_pass, a == 0, False)
-                product(acc[:], columns(pros_q, P * g, P), columns(wp_q[b], 0, W), False, True)
-                gate[b, g] = ring.tile([P, 4, P], F32, name=f"gate{b}{g}", tag="gate", bufs=GATE_BUFS, align_bytes=64)
-                nc.scalar.activation(out=gate[b, g][:], in_=acc[:].rearrange("m (p t) -> m t p", t=4), func=ACT.Sigmoid)
+                    product(acc[:], columns(st_q[a], P * blk, P), ug_pass, a == 0, False)
+                product(acc[:], columns(pros_q, P * blk, P), columns(wp_q[b], 0, W), False, True)
+                gate[b, blk] = ring.tile([P, 4, P], F32, name=f"gate{b}{blk}", tag="gate", bufs=GATE_BUFS, align_bytes=64)
+                nc.scalar.activation(out=gate[b, blk][:], in_=acc[:].rearrange("m (p t) -> m t p", t=4), func=ACT.Tanh, scale=0.5)
 
         faded = {}
         for b in range(2):
             for t in range(4):
                 acc = bank(f"keep{b}{t}")
-                for g in range(4):
-                    nc.tensor.transpose(acc[:, P * g : P * (g + 1)], gate[b, g][:, t, :], ident[:])
+                for blk in range(4):
+                    nc.tensor.transpose(acc[:, P * blk : P * (blk + 1)], gate[b, blk][:, t, :], ident[:])
                 faded[b, t] = held_tile([P, M], F32, f"faded{b}{t}")
-                nc.vector.tensor_tensor(out=faded[b, t][:], in0=acc[:], in1=st_raw[b][:, t, :], op=MULT)
+                nc.vector.scalar_tensor_tensor(
+                    out=faded[b, t][:], in0=acc[:], scalar=1.0, in1=st_raw[b][:, t, :], op0=ADD, op1=MULT
+                )
             for t in range(4):
                 acc = bank(f"cand_acc{b}{t}")
                 for a in range(2):
@@ -224,7 +229,7 @@ def tile_list_voice_state_step_kernel(
             planes = scratch_tile([P, 4, HALF], BF16, f"new{b}{s}")
             for t in range(4):
                 nc.vector.scalar_tensor_tensor(
-                    out=planes[:, t, :], in0=cand[b][:, t, cols], scalar=gain_sb[:, b, t : t + 1],
+                    out=planes[:, t, :], in0=cand[b][:, t, cols], scalar=gain2[:, b, t : t + 1],
                     in1=faded[b, t][:, cols], op0=MULT, op1=ADD,
                 )
             woven = rounded_tile(4 * HALF, f"new_bf{b}{s}")

from contextlib import ExitStack

import concourse.mybir as mybir
from concourse.masks import make_identity

T, S, M = 2048, 1024, 512
K, F, H, N = 512, 512, 1024, 512
FLOPS = 2 * (K * H * S + 2 * H * H * M + F * H * M + H * N * M)

F32 = mybir.dt.float32
BF16 = mybir.dt.bfloat16
I32 = mybir.dt.int32
U32 = mybir.dt.uint32
U16 = mybir.dt.uint16
U8 = mybir.dt.uint8
FP8X4 = mybir.dt.float8_e4m3fn_x4
FP4X4 = mybir.dt.float4_e2m1fn_x4
ACT = mybir.ActivationFunctionType
MULT = mybir.AluOpType.mult
ADD = mybir.AluOpType.add

P = 128
W = 512
HALF = M // 2
LIST_COLS = W // 16
RAW_BUFS = 7
ROUNDED_BUFS = 6
SCRATCH_BUFS = 7
GATE_BUFS = 4


def tile_list_voice_state_step_kernel(
    tc, tab_words, tab_scales, offs, offs2, wgt, wc_words, wc_scales, ug_words, ug_scales,
    us, wp, wo, st, pros, gain, out_0, out_1, out_2,
):
    nc = tc.nc
    with ExitStack() as ctx:
        held = ctx.enter_context(tc.tile_pool(name="held", bufs=1))
        ring = ctx.enter_context(tc.tile_pool(name="ring", bufs=1))
        psum = ctx.enter_context(tc.psum_pool(name="psum", bufs=1))

        def held_tile(shape, dtype, name):
            return held.tile(shape, dtype, name=name, align_bytes=64)

        def raw_tile(shape, dtype, name):
            return ring.tile(shape, dtype, name=name, tag="raw", bufs=RAW_BUFS, align_bytes=64)

        def rounded_tile(width, name):
            return ring.tile([P, width], BF16, name=name, tag="rounded", bufs=ROUNDED_BUFS, align_bytes=64)

        def scratch_tile(shape, dtype, name):
            return ring.tile(shape, dtype, name=name, tag="scratch", bufs=SCRATCH_BUFS, align_bytes=64)

        def bank(name):
            return psum.tile([P, W], F32, name=name, tag="bank", bufs=8)

        def load_pass(make, src, a, b, name):
            tile = make([P, 4, W], F32, name)
            nc.sync.dma_start(out=tile[:], in_=src[W * a : W * (a + 1), W * b : W * (b + 1)].rearrange("(p j) c -> p j c", j=4))
            return tile

        def load_scale_rows(tile, src):
            for q in range(4):
                nc.sync.dma_start(out=tile[32 * q : 32 * q + 4, :].bitcast(I32), in_=src[0, 4 * q : 4 * q + 4, :].bitcast(I32))

        tab_sc = held_tile([P, T], U8, "tab_sc")
        wc_sc = held_tile([P, H], U8, "wc_sc")
        ug_sc = held_tile([P, H], U8, "ug_sc")
        gain_sb = held_tile([P, 2, 4], F32, "gain_sb")
        wgt_sb = held_tile([P, M], F32, "wgt_sb")
        wc_raw = held_tile([P, 2 * H], U8, "wc_raw")
        ug_raw = held_tile([P, 2 * H], I32, "ug_raw")
        tab_raw = raw_tile([P, T], I32, "tab_raw")
        frames = held.tile([P, S // 16], U16, name="frames")
        picks = held.tile([P, M // 16], U16, name="picks")
        for scale_tile in (tab_sc, wc_sc, ug_sc):
            nc.gpsimd.memset(scale_tile[:].bitcast(I32), 0)
        ident = held_tile([P, P], F32, "ident")
        make_identity(nc, ident[:])

        nc.sync.dma_start(frames[:], offs)
        nc.sync.dma_start(out=wc_raw[:].bitcast(I32), in_=wc_words[0].bitcast(I32))
        nc.sync.dma_start(picks[:], offs2)
        load_scale_rows(tab_sc, tab_scales)
        nc.sync.dma_start(out=tab_raw[:], in_=tab_words[0].rearrange("p t i -> p (t i)").bitcast(I32))
        st_raw = [load_pass(held_tile, st, 0, 0, "st0")]
        load_scale_rows(wc_sc, wc_scales)
        st_raw.append(load_pass(held_tile, st, 1, 0, "st1"))
        nc.sync.dma_start(out=wgt_sb[:], in_=wgt)
        pros_raw = load_pass(raw_tile, pros, 0, 0, "pros")
        wp_raw = [load_pass(raw_tile, wp, 0, 0, "wp0")]
        nc.sync.dma_start(
            out=ug_raw[:].rearrange("p (a c) -> p a c", a=2), in_=ug_words.rearrange("a p c i -> p a (c i)").bitcast(I32)
        )
        for q in range(4):
            nc.sync.dma_start(
                out=ug_sc[32 * q : 32 * q + 8, :].bitcast(I32), in_=ug_scales[:, 4 * q : 4 * q + 4, :].bitcast(I32)
            )
        wp_raw.append(load_pass(raw_tile, wp, 0, 1, "wp1"))
        us_raw = [[load_pass(raw_tile, us, a, b, f"us{a}{b}") for a in range(2)] for b in range(2)]
        nc.sync.dma_start(out=gain_sb[:], in_=gain.rearrange("(b p t) -> p b t", b=2, t=4))
        wo_raw = [load_pass(raw_tile, wo, b, 0, f"wo{b}") for b in range(2)]

        on_vector, on_scalar = nc.vector.tensor_copy, nc.scalar.copy

        def halved_on_scalar(out, in_):
            nc.scalar.activation(out=out, in_=in_, func=ACT.Copy, scale=0.5)

        def weave(copy, out, planes):
            copy(out=out.rearrange("p (c i j) -> p c j i", i=4, j=4), in_=planes.rearrange("p j (c i) -> p c j i", i=4))

        def weave_and_deal(copy, out, planes):
            copy(out=out.rearrange("p (t m j) -> p m j t", t=4, j=4), in_=planes.rearrange("p j (m t) -> p m j t", t=4))

        def quantise(rounded, width, name):
            codes = held_tile([P, width], U32, name + "_codes")
            scales = held_tile([P, width], U8, name + "_scales")
            nc.vector.quantize_mx(out=codes[:].bitcast(FP8X4), scales=scales[:], in_=rounded[:])
            return codes, scales

        def prepare(layout, copy, planes, name):
            rounded = rounded_tile(4 * W, name + "_bf")
            layout(copy, rounded[:], planes[:])
            return quantise(rounded, W, name)

        def product(acc, lhs, rhs, start, stop):
            nc.tensor.matmul_mx(
                out=acc, lhsT=lhs[0].bitcast(FP8X4), lhsT_scale=lhs[1], rhs=rhs[0].bitcast(FP8X4), rhs_scale=rhs[1],
                start=start, stop=stop,
            )

        def columns(operand, first, count):
            return operand[0][:, first : first + count], operand[1][:, first : first + count]

        def deal_wc(b):
            codes = held_tile([P, 2 * W], U8, f"wc_codes{b}")
            nc.vector.tensor_copy(
                out=codes[:].bitcast(U16).rearrange("p (t m) -> p t m", t=4),
                in_=wc_raw[:, 2 * W * b : 2 * W * (b + 1)].bitcast(U16).rearrange("p (m t) -> p t m", t=4),
            )
            scales = held_tile([P, W], U8, f"wc_scales{b}")
            nc.vector.tensor_copy(
                out=scales[:].rearrange("p (t m) -> p t m", t=4),
                in_=wc_sc[:, W * b : W * (b + 1)].rearrange("p (m t) -> p t m", t=4),
            )
            return codes, scales

        def gather_frames(f):
            offsets = frames[:, LIST_COLS * f : LIST_COLS * (f + 1)]
            codes = held_tile([P, W], U32, f"v_codes{f}")
            nc.vector.tensor_copy(out=codes[:], in_=tab_raw[:].bitcast(U32).indirect(offsets))
            scales = held_tile([P, W], U8, f"v_scales{f}")
            nc.vector.tensor_copy(out=scales[:], in_=tab_sc[:].indirect(offsets))
            return codes, scales

        wc_q, v_q = [], []
        for i in range(2):
            wc_q.append(deal_wc(i))
            v_q.append(gather_frames(i))

        st_bf = held_tile([P, 8 * W], BF16, "st_bf")
        for a, copy in enumerate((on_scalar, on_vector)):
            weave(copy, st_bf[:, 4 * W * a : 4 * W * (a + 1)], st_raw[a][:])
        st_both = quantise(st_bf, 2 * W, "st")
        st_q = [columns(st_both, W * a, W) for a in range(2)]
        pros_q = prepare(weave, on_scalar, pros_raw, "pros")
        wp_q = [prepare(weave, copy, wp_raw[b], f"wp{b}") for b, copy in enumerate((on_vector, on_scalar))]
        us_q = [
            [prepare(weave_and_deal, copy, us_raw[b][a], f"us{a}{b}") for a, copy in enumerate((on_scalar, on_vector))]
            for b in range(2)
        ]
        wo_q = [prepare(weave_and_deal, halved_on_scalar, wo_raw[b], f"wo{b}") for b in range(2)]
        gain2 = held_tile([P, 2, 4], F32, "gain2")
        nc.scalar.activation(out=gain2[:], in_=gain_sb[:], func=ACT.Copy, scale=2.0)

        cand = [held_tile([P, 4, M], F32, f"cand{b}") for b in range(2)]
        for b in range(2):
            for t in range(4):
                h = scratch_tile([P, S], F32, f"h{b}{t}")
                for f in range(2):
                    acc = bank(f"h_acc{b}{t}{f}")
                    nc.tensor.matmul_mx(
                        out=acc[:],
                        lhsT=wc_q[b][0][:, 2 * P * t : 2 * P * (t + 1)].bitcast(FP4X4),
                        lhsT_scale=wc_q[b][1][:, P * t : P * (t + 1)],
                        rhs=v_q[f][0][:].bitcast(FP8X4),
                        rhs_scale=v_q[f][1][:],
                        start=True,
                        stop=True,
                    )
                    nc.scalar.copy(out=h[:, W * f : W * (f + 1)], in_=acc[:])
                nc.vector.tensor_tensor(out=cand[b][:, t, :], in0=h[:].indirect(picks[:]), in1=wgt_sb[:], op=MULT)

        gate = {}
        for b in range(2):
            for blk in range(4):
                acc = bank(f"gate_acc{b}{blk}")
                for a in range(2):
                    ug_pass = ug_raw[:, H * a + W * b : H * a + W * (b + 1)], ug_sc[4 * a :, W * b : W * (b + 1)]
                    product(acc[:], columns(st_q[a], P * blk, P), ug_pass, a == 0, False)
                product(acc[:], columns(pros_q, P * blk, P), columns(wp_q[b], 0, W), False, True)
                gate[b, blk] = ring.tile([P, 4, P], F32, name=f"gate{b}{blk}", tag="gate", bufs=GATE_BUFS, align_bytes=64)
                nc.scalar.activation(out=gate[b, blk][:], in_=acc[:].rearrange("m (p t) -> m t p", t=4), func=ACT.Tanh, scale=0.5)

        faded = {}
        for b in range(2):
            for t in range(4):
                acc = bank(f"keep{b}{t}")
                for blk in range(4):
                    nc.tensor.transpose(acc[:, P * blk : P * (blk + 1)], gate[b, blk][:, t, :], ident[:])
                faded[b, t] = held_tile([P, M], F32, f"faded{b}{t}")
                nc.vector.scalar_tensor_tensor(
                    out=faded[b, t][:], in0=acc[:], scalar=1.0, in1=st_raw[b][:, t, :], op0=ADD, op1=MULT
                )
            for t in range(4):
                acc = bank(f"cand_acc{b}{t}")
                for a in range(2):
                    product(acc[:], columns(us_q[b][a], P * t, P), st_q[a], a == 0, a == 1)
                nc.vector.tensor_tensor(out=cand[b][:, t, :], in0=acc[:], in1=cand[b][:, t, :], op=ADD)
                nc.scalar.activation(out=cand[b][:, t, :], in_=cand[b][:, t, :], func=ACT.Tanh)

        y_scales = held_tile([P, M], U8, "y_scales")
        y_rows = out_0.rearrange("(p t) m -> p t m", t=4)
        y_words = out_1[0].rearrange("p m t -> p (m t)").bitcast(I32)
        new_q = {}

        def blend(b, s, copy):
            cols = slice(HALF * s, HALF * (s + 1))
            planes = scratch_tile([P, 4, HALF], BF16, f"new{b}{s}")
            for t in range(4):
                nc.vector.scalar_tensor_tensor(
                    out=planes[:, t, :], in0=cand[b][:, t, cols], scalar=gain2[:, b, t : t + 1],
                    in1=faded[b, t][:, cols], op0=MULT, op1=ADD,
                )
            woven = rounded_tile(4 * HALF, f"new_bf{b}{s}")
            weave(copy, woven[:], planes[:])
            new_q[b, s] = quantise(woven, HALF, f"new{b}{s}")

        def finish(s, plane_copies, rounding_copy):
            cols = slice(HALF * s, HALF * (s + 1))
            y = scratch_tile([P, 4, HALF], F32, f"y{s}")
            for t, copy in enumerate(plane_copies):
                acc = bank(f"y_acc{s}{t}")
                for b in range(2):
                    product(acc[:, 0:HALF], columns(wo_q[b], P * t, P), columns(new_q[b, s], 0, HALF), b == 0, b == 1)
                copy(out=y[:, t, :], in_=acc[:, 0:HALF])
            nc.sync.dma_start(out=y_rows[:, :, cols], in_=y[:])
            rounded = rounded_tile(4 * HALF, f"y_bf{s}")
            weave(rounding_copy, rounded[:], y[:])
            y_codes = held_tile([P, HALF], I32, f"y_codes{s}")
            nc.vector.quantize_mx(out=y_codes[:].bitcast(FP8X4), scales=y_scales[:, cols], in_=rounded[:])
            nc.sync.dma_start(out=y_words[:, cols], in_=y_codes[:])

        blend(0, 0, on_scalar)
        blend(1, 0, on_scalar)
        blend(0, 1, on_scalar)
        finish(0, (on_scalar,) * 4, on_scalar)
        blend(1, 1, on_vector)
        finish(1, (on_scalar, on_vector) * 2, on_vector)
        for q in range(4):
            nc.scalar.dma_start(
                out=out_2[0, 4 * q : 4 * q + 4, :].bitcast(I32), in_=y_scales[32 * q : 32 * q + 4, :].bitcast(I32)
            )
